import numpy as np, ml_dtypes
CORES = [51,54,179,182]
N = 4
BF = ml_dtypes.bfloat16
def gentries(a):
    return np.ascontiguousarray(a.reshape(8, 16, -1).transpose(0, 2, 1)).reshape(8, -1)
def gtable(e):
    e = np.asarray(e); return np.ascontiguousarray(e.reshape(8, -1, 16).transpose(0, 2, 1)).reshape(128, -1).astype(np.int32)
V, B, BITS, RO = 1536, 512, 12, 5
M = N * B
W = M + V - B
C = 2 ** BITS
def seen(q, p):
    bq = np.ascontiguousarray(q[..., :B].transpose(1, 2, 0, 3)).reshape(8, 16, M)
    bp = np.ascontiguousarray(p[..., :B].transpose(1, 0, 2)).reshape(8, M)
    gs, qps, qgs = [], [], []
    for a in range(N):
        wq = np.concatenate([bq, q[a, :, :, B:]], axis=2); wp = np.concatenate([bp, p[a, :, B:]], axis=1)
        g = np.take_along_axis(wp, p[a], 1)
        gs.append(g); qps.append(np.take_along_axis(wq, p[a][:, None, :], 2)); qgs.append(np.take_along_axis(wq, g[:, None, :], 2))
    return np.stack(gs), np.stack(qps), np.stack(qgs)
def dots(am, z):
    return np.matmul(am.transpose(0, 1, 3, 2), z)
def codes(am, t, z):
    return np.add.reduce(np.where(dots(am, z)[:, :, :BITS] > t[:, :, :BITS], 2 ** np.arange(BITS)[:, None], 0), axis=2)
def forest(rng):
    span = rng.choice(np.array([2, 16, B, M]), (8, 1)); i = np.arange(M)
    o = np.argsort(rng.random((8, M)), axis=1); back = np.minimum(i, (rng.random((8, M)) * span).astype(np.int64) + 1)
    pb = np.zeros((8, M), np.int64); np.put_along_axis(pb, o, np.take_along_axis(o, i - np.where(rng.random((8, M)) < 0.02, 0, back), 1), 1)
    h = V - B; i = np.arange(h); span = rng.choice(np.array([2, 16, B, h]), (N, 8, 1))
    o = np.argsort(rng.random((N, 8, h)), axis=2); back = np.minimum(i, (rng.random((N, 8, h)) * span).astype(np.int64) + 1)
    pi = np.zeros((N, 8, h), np.int64); np.put_along_axis(pi, o, np.take_along_axis(o, i - np.where(rng.random((N, 8, h)) < 0.02, 0, back), 2), 2)
    pi = np.where(rng.random((N, 8, h)) < 0.5, rng.integers(0, M, (N, 8, h)), M + pi)
    return np.concatenate([pb.reshape(8, N, B).transpose(1, 0, 2), pi], axis=2)
def parts(rng):
    amp = rng.choice(np.array([8, 24, 64]), (N, 8, 1, V))
    q = 64 + np.floor((2 * rng.random((N, 8, 16, V)) - 1) * amp).astype(np.int64); q = np.clip(q, 0, 127)
    am = rng.integers(-1, 2, (N, 8, 16, 16))
    t = 128 * np.add.reduce(am, axis=2)[..., None] + rng.integers(-30, 31, (N, 8, 16, 1))
    c = np.clip(rng.choice(np.array([0, 8, 24, 64, 111]), (N, 8, 1, C)) + rng.integers(0, 17, (N, 8, 16, C)), 0, 127)
    return q, forest(rng), am, t, c
def pack(q, p, am, t, c):
    big = np.zeros((N, 128, 128), np.float32)
    for h in range(8): big[:, 16 * h:16 * h + 16, 16 * h:16 * h + 16] = am[:, h]
    return {"q": np.ascontiguousarray(q).reshape(N, 128, V).astype(np.float32).astype(BF), "par": np.stack([gtable(a) for a in p]), "amat": big.astype(BF),
            "clr": np.ascontiguousarray(c).reshape(N, 128, C).astype(np.float32).astype(BF), "th": np.ascontiguousarray(t).reshape(N, 128, 1).astype(np.int32)}
def setup_inputs(rng):
    return pack(*parts(rng))
def setup_inputs_edge(rng):
    q, p, am, t, c = parts(rng); q = 64 + rng.integers(-6, 7, q.shape)
    g, qp, qg = seen(q, p); s = dots(am, q + qg); low = rng.integers(0, 2, (N, 8, 16, 1)); low[:, :, 0] = 0; low[:, :, 1] = 1
    t = np.take_along_axis(s, rng.integers(0, V, (N, 8, 16, 1)), 3) - low
    code = codes(am, t, q + qg); gap = np.abs(q - qg)
    for a in range(N):
        for h in range(8):
            w = np.full(C, -1); w[code[a, h]] = np.arange(V); k = np.nonzero(w >= 0)[0]; n = np.arange(len(k))
            e = gap[a, h][:, w[k]].copy(); x = np.argmax(e, axis=0)
            e[x, n] = e[x, n] - ((rng.random(len(k)) < 0.5) & (e[x, n] > 0)).astype(np.int64)
            c[a, h][:, k] = e
    return pack(q, p, am, t, c)
def setup_inputs_chain(rng):
    q, p, am, t, c = parts(rng); k = np.arange(B)
    for r in range(N):
        p[r, 0::2, :B] = (r + 1) % N * B + (k + (r == N - 1)) % B
        p[r, 1::2, :B] = (r - 1) * B + k if r else np.where(k > 0, (N - 1) * B + k - 1, 0)
        p[r, :, B:] = M + np.arange(V - B) - 1; p[r, :, B] = r * B + B - 1
    c[:, 0:2] = 127; c[:, 2:4] = 0
    return pack(q, p, am, t, c)
def setup_inputs_alike(rng):
    q, p, am, t, c = parts(rng)
    p[:, 0:2, :B] = rng.choice(np.array([0, B - 1, B, M - 1]), (N, 2, B)); p[:, 0:2, B:] = rng.choice(np.array([0, M - 1, M, W - 1]), (N, 2, V - B))
    for r in range(N):
        p[r, 2, :B] = r * B + np.arange(B); p[r, 2, B:] = M + np.arange(V - B)
    p[:, 3, B:] = rng.integers(M, W, (N, V - B)); p[:, 4, B:] = rng.integers(0, M, (N, V - B))
    t[:, 5] = -4096; c[:, 5, :, C - 1] = rng.integers(20, 60, (N, 16)); t[:, 6] = 4096; c[:, 6, :, 0] = rng.integers(20, 60, (N, 16))
    q[:, 7] = 127 * rng.integers(0, 2, (N, 16, V)); one = np.arange(16)[:, None] == rng.integers(0, 16, (N, 1, C))
    c[:, 7] = 127 - (one & (rng.random((N, 1, C)) < 0.7)).astype(np.int64)
    return pack(q, p, am, t, c)
def setup_inputs_spread(rng):
    q, p, am, t, c = parts(rng)
    q = np.clip(np.floor(np.exp2(7.5 * rng.random((N, 8, 1, V))) * rng.random((N, 8, 16, V))).astype(np.int64), 0, 127)
    am = am * (rng.random((N, 8, 16, 16)) < rng.choice(np.array([0.1, 0.4, 1.0]), (N, 8, 1, 16)))
    t = np.floor(np.exp2(12 * rng.random((N, 8, 16, 1)) ** 1.5)).astype(np.int64) * rng.choice(np.array([-1, 1]), (N, 8, 16, 1)); t = np.clip(t, -4096, 4096)
    c = np.clip(np.floor(np.exp2(8 * rng.random((N, 8, 1, C))) * (0.5 + rng.random((N, 8, 16, C)))).astype(np.int64), 0, 127)
    return pack(q, p, am, t, c)
def setup_inputs_large(rng):
    q, p, am, t, c = parts(rng)
    q[:, :5] = 127 - np.floor(rng.random((N, 5, 16, V)) * rng.choice(np.array([1, 4, 16, 40]), (N, 5, 1, V))).astype(np.int64)
    cut = rng.integers(0, 3, (N, 5, 1, 16)); cut[:, 4] = 4; less = -rng.integers(0, 2, (N, 5, 16, 16)); less[:, 4] = -1
    sign = rng.choice(np.array([-1, 1]), (N, 5, 1, 16)); sign[:, 0] = 1; sign[:, 1] = -1
    am[:, :5] = sign * np.where(np.argsort(rng.random((N, 5, 16, 16)), axis=2) < cut, less, 1)
    for h in range(5, 8):
        a = int(rng.integers(0, N)); b = (a + 1) % N; ka = int(rng.integers(0, B)); kb = int(rng.integers(0, B))
        p[:, h] = a * B + ka; p[a, h, ka] = b * B + kb; p[b, h, kb] = b * B + kb
        am[:, h] = np.eye(16, dtype=np.int64); mid = rng.integers(32, 96, (N, 16, 1))
        for r in range(N):
            w = rng.permutation(np.concatenate([np.arange(C), rng.integers(0, C, max(V - C, 0))]))[:V]
            bit = (w[None, :] >> np.arange(16)[:, None]) & 1; bit[BITS:] = rng.integers(0, 2, (16 - BITS, V)); u = rng.random((16, V))
            q[r, h] = np.where(bit == 1, mid[r] + 1 + np.floor(u * (127 - mid[r])).astype(np.int64), np.floor(u * (mid[r] + 1)).astype(np.int64))
        t[:, h] = mid + q[b, h, :, kb][None, :, None]
    g, qp, qg = seen(q, p); s = np.take_along_axis(dots(am, q + qg), rng.integers(0, V, (N, 8, 16, 1)), 3)
    low = np.where((s & 3) == 1, 1, np.where((s & 3) == 3, 0, rng.integers(0, 2, s.shape)))
    t[:, :5] = (s - low)[:, :5]
    c[:] = 127 * rng.integers(0, 2, (N, 8, 1, C))
    return pack(q, p, am, t, c)
def check_inputs(d):
    bad = []
    for k in ("q", "clr"):
        x = np.asarray(d[k]).astype(np.float32)
        if not np.all((x >= 0) & (x <= 127) & (x == np.floor(x))): bad.append("numbers of " + k)
    if np.min(d["th"]) < -4096 or np.max(d["th"]) > 4096: bad.append("range of th")
    x = np.asarray(d["amat"]).astype(np.float32); same = np.arange(128)[:, None] // 16 == np.arange(128)[None, :] // 16
    if not np.all((x == 0) | (same & ((x == 1) | (x == -1)))): bad.append("numbers of amat")
    if np.min(d["par"]) < 0 or np.max(d["par"]) > W - 1: bad.append("range of par")
    if np.max(np.stack([gentries(a) for a in d["par"]])[:, :, :B]) > M - 1: bad.append("parents of border columns")
    return bad
def reference(q, par, amat, clr, th):
    x = q.astype(np.float32).astype(np.int64).reshape(N, 8, 16, V); p = np.stack([gentries(a) for a in par]).astype(np.int64)
    big = amat.astype(np.float32).astype(np.int64); am = np.stack([big[:, 16 * h:16 * h + 16, 16 * h:16 * h + 16] for h in range(8)], axis=1)
    c = clr.astype(np.float32).astype(np.int64).reshape(N, 8, 16, C); t = th.astype(np.int64).reshape(N, 8, 16, 1)
    for rnd in range(RO):
        g, xp, xg = seen(x, p)
        code = codes(am, t, x + xg)
        room = np.take_along_axis(c, code[:, :, None, :], 3)
        ok = np.all(room >= np.abs(x - xg), axis=2)
        p = np.where(ok, g, p); x = np.where(ok[:, :, None, :], x, (x + xp) >> 1)
    return {"yq": x.reshape(N, 128, V).astype(np.float32).astype(BF), "yp": np.stack([gtable(a) for a in p]).astype(np.float32)}

@@ -1,0 +1,334 @@
+from concourse.bass import DstId, RemoteDMATransfer
+from concourse.mybir import AluOpType as ALU, AxisListType, ActivationFunctionType as AF
+
+N, V, B, RO, C = 4, 1536, 512, 5, 4096
+M = N * B
+OFF = B
+INN = OFF + M
+DUP = INN + V - B
+WW = DUP + V - B
+BIG = 8192.0
+
+SCRATCH = {}
+for _r in range(RO):
+    SCRATCH["w%d" % _r] = ("sbuf", [128, WW], "bfloat16")
+    SCRATCH["pw%d" % _r] = ("sbuf", [128, 192], "float32")
+for _n, _w, _d in [
+    ("fin", V, "bfloat16"), ("yqs", V, "bfloat16"), ("pfin", 96, "float32"), ("yps", 96, "float32"),
+    ("clrs", C, "bfloat16"), ("am", 128, "bfloat16"), ("thi", 1, "int32"), ("pari", 96, "int32"),
+    ("oh", 3072, "bfloat16"), ("msk", V, "bfloat16"), ("cand", V, "float16"), ("dd", V, "bfloat16"),
+    ("sg", V, "bfloat16"), ("ae", V, "bfloat16"), ("viol", V, "bfloat16"),
+    ("ab0", B, "float32"), ("ab1", B, "float32"), ("ab2", B, "float32"),
+    ("ah0", B, "float16"), ("ah1", B, "float16"), ("ah2", B, "float16"),
+    ("u4", 96, "uint16"), ("up", 96, "uint16"), ("uh", 96, "uint16"), ("uc", 96, "uint16"), ("us", 96, "uint16"),
+    ("dh", 96, "float32"), ("sl", 96, "float32"), ("okf", 96, "float32"), ("tt", 96, "float32"),
+    ("pci", 1, "int32"), ("rci", 1, "int32"), ("pcol", 1, "float32"), ("rcol", 1, "float32"), ("gcol", 1, "float32"),
+    ("wcol", 1, "float32"), ("b0", 1, "float32"), ("b1", 1, "float32"), ("one", 1, "bfloat16"),
+    ("x143", 144, "float32"), ("x16", 256, "bfloat16"), ("two", 16, "float32"), ("zero", 16, "float32"),
+    ("pk2", 16, "float32"), ("pk3", 16, "float32"),
+    ("zc", 144, "bfloat16"), ("zo", 144, "float16"), ("zp", 144, "bfloat16"), ("zn", 144, "bfloat16"),
+    ("idp", 128, "bfloat16"), ("idn", 128, "bfloat16"), ("uc1", 96, "bfloat16"), ("uc2", 96, "bfloat16"),
+]:
+    SCRATCH[_n] = ("sbuf", [128, _w], _d)
+for _n in ["ps0", "ps1", "ps2", "pe0", "pe1", "pe2", "pkb", "pki"]:
+    SCRATCH[_n] = ("psum", [128, 512], "float32")
+
+LOADS = ["par", "qb", "clr", "qi", "am", "th", "qdb", "qdi"]
+SEMAPHORES = ["sv", "sa", "sp", "sgp"] + ["ld_" + x for x in LOADS] + ["st%d" % i for i in range(5)]
+for _r in range(RO):
+    SEMAPHORES += ["ap%d" % _r, "aq%d" % _r, "lp%d" % _r, "lq%d" % _r, "db%d" % _r, "di%d" % _r]
+
+CFG = {"T2_2_1", "T2_4_2", "T7_0_2", "T7_2_0", "T7_3_0", "T8_0_0", "T8_2_0", "fin2"}
+ORDER = [8,9,10,1,3,5,0,6,7,2,4,13,17,18,14,21,22,38,41,16,15,19,26,33,72,43,11,39,40,12,23,71,42,27,20,28,24,31,32,45,35,46,25,75,44,79,73,47,48,36,81,82,78,49,80,50,29,51,76,37,52,53,54,83,55,56,57,30,34,74,84,58,60,85,86,91,77,59,87,61,92,93,88,89,94,63,62,65,64,66,68,67,69,96,90,111,110,97,95,112,113,99,100,114,98,101,115,117,116,103,102,105,104,106,118,139,107,108,140,119,120,143,121,122,123,125,124,144,70,109,147,126,128,148,127,129,151,149,146,131,130,133,142,141,134,132,152,136,153,180,178,179,181,135,137,159,154,160,150,161,145,155,184,156,183,162,157,163,158,182,164,185,165,168,186,167,166,169,188,187,171,170,173,174,172,207,175,208,189,191,211,193,213,190,215,192,194,212,216,176,219,217,218,195,220,196,222,197,138,177,209,227,199,201,202,198,221,200,246,204,203,228,223,214,224,229,205,230,225,226,231,210,249,232,233,247,235,236,250,234,251,252,237,253,239,241,238,242,275,254,276,240,255,243,279,283,280,284,244,281,256,257,258,287,206,245,288,259,260,261,290,262,264,248,289,285,282,263,291,265,295,267,266,269,268,270,296,271,293,298,286,292,300,297,272,314,301,273,294,277,299,317,278,303,304,315,302,305,319,307,306,309,308,310,345,344,318,311,352,348,321,322,353,349,312,324,313,274,350,351,320,326,325,356,327,328,357,323,364,359,355,329,354,365,360,367,362,330,332,358,361,331,333,369,366,335,334,337,336,338,370,363,368,316,346,347,371,372,373,339,374,375,340,377,376,380,381,378,386,379,382,342,384,343,341,385,387,383]
+
+
+def build_ops(g, T, topo, core, rank, cfg):
+    ops = []
+
+    def op(name, eng, kind, n, reads, writes, fn, sem=None):
+        ops.append(dict(name=name, eng=eng, kind=kind, n=n, reads=reads, writes=writes, fn=fn, sem=sem))
+
+    vec, act, pe = g.vector, g.scalar, g.tensor
+    W = [T["w%d" % r] for r in range(RO)]
+    PW = [T["pw%d" % r] for r in range(RO)]
+    own0 = OFF + B * rank
+
+    def dma(name, eng, out, in_, reads, writes, sem, n):
+        q = g.sync if eng == "s" else g.scalar
+        op(name, eng, "dma", n, reads, writes, lambda: q.dma_start(out, in_), sem)
+
+    dma("l_par", "s", T.pari[:], T.par[:], [], ["pari"], "ld_par", 0)
+    dma("l_qb", "a", W[0][:, own0:own0 + B], T.q[:, 0:B], [], [("w", 0, 0)], "ld_qb", 300)
+    dma("l_qi", "s", W[0][:, INN:DUP], T.q[:, B:V], ["ld1"], [("w", 0, 1), ("w", 0, 2)], "ld_qi", 900)
+    dma("l_am", "a", T.am[:], T.amat[:], [], ["am"], "ld_am", 500)
+    dma("l_clr", "s", T.clrs[:], T.clr[:], [], ["clrs"], "ld_clr", 4000)
+    dma("l_th", "a", T.thi[:], T.th[:], [], ["thi"], "ld_th", 600)
+    dma("l_qdb", "s", W[0][:, 0:B], T.q[:, 0:B], [], [("wd", 0, 0)], "ld_qdb", 4500)
+    dma("l_qdi", "s", W[0][:, DUP:WW], T.q[:, B:V], [], [("wd", 0, 1)], "ld_qdi", 5000)
+
+    def gp(name, n, w, fn):
+        op(name, "g", "iota", n, [], [w], fn)
+
+    def vs(name, n, reads, writes, fn):
+        op(name, "v", "op", n, reads, writes, fn)
+
+    gp("i_p", 1, "pci", lambda: g.iota(T.pci[:], [[0, 1]], 0, 1))
+    gp("i_16", 256, "x16", lambda: g.iota(T.x16[:], [[0, 16], [1, 16]], 0, 0, allow_small_or_imprecise_dtypes=True))
+    gp("i_143", 144, "x143", lambda: g.iota(T.x143[:], [[1, 144]], -15, 0, allow_small_or_imprecise_dtypes=True))
+    gp("i_u1", 32, "uc1b", lambda: g.iota(T.uc1[:, 0:32], [[16, 32]], -OFF - 1024, 0, allow_small_or_imprecise_dtypes=True))
+    gp("i_u2", 64, "uc1i", lambda: g.iota(T.uc1[:, 32:96], [[16, 64]], DUP - OFF - 1024, 0, allow_small_or_imprecise_dtypes=True))
+    vs("c_two", 16, [], ["two"], lambda: vec.memset(T.two[:], 2.0))
+    vs("c_zero", 16, [], ["zero"], lambda: vec.memset(T.zero[:], 0.0))
+    vs("c_one", 1, [], ["one"], lambda: vec.memset(T.one[:], 1.0))
+    vs("c_pk2", 16, ["two", "zero"], ["pk2"],
+       lambda: vec.tensor_tensor_scan(T.pk2[:], T.two[:], T.zero[:], 0.25, ALU.mult, ALU.add))
+    vs("c_rci", 1, ["pci"], ["rci"], lambda: vec.tensor_scalar(T.rci[:], T.pci[:], 15, None, ALU.bitwise_and))
+    vs("c_rcol", 1, ["rci"], ["rcol"], lambda: vec.tensor_copy(T.rcol[:], T.rci[:]))
+    vs("c_pcol", 1, ["pci"], ["pcol"], lambda: vec.tensor_copy(T.pcol[:], T.pci[:]))
+    vs("c_gcol", 1, ["pcol", "rcol"], ["gcol"], lambda: vec.tensor_tensor(T.gcol[:], T.pcol[:], T.rcol[:], ALU.subtract))
+    vs("c_oh0", 128, ["x16", "rcol"], ["oh0"], lambda: vec.tensor_scalar(T.oh[:, 0:256], T.x16[:], T.rcol[:], None, ALU.is_equal))
+    vs("c_oh1", 128, ["oh0"], ["oh1"], lambda: vec.tensor_copy(T.oh[:, 256:512], T.oh[:, 0:256]))
+    vs("c_oh2", 256, ["oh0", "oh1"], ["oh2"], lambda: vec.tensor_copy(T.oh[:, 512:1024], T.oh[:, 0:512]))
+    vs("c_oh3", 512, ["oh0", "oh1", "oh2"], ["ohb"], lambda: vec.tensor_copy(T.oh[:, 1024:2048], T.oh[:, 0:1024]))
+    op("c_oh4", "a", "op", 1024, ["oh0", "oh1", "oh2"], ["ohi"],
+       lambda: act.activation(T.oh[:, 2048:3072], T.oh[:, 0:1024], AF.Copy))
+    vs("c_pk3", 32, ["pk2", "oh0"], ["pk3"], lambda: vec.tensor_tensor(T.pk3[:], T.pk2[:], T.oh[:, 0:16], ALU.mult))
+    vs("c_wcol", 16, ["pk3"], ["wcol"], lambda: vec.tensor_reduce(T.wcol[:], T.pk3[:, 0:12], AxisListType.X, ALU.add))
+    vs("c_zo", 144, ["x143", "gcol"], ["zo"], lambda: vec.tensor_scalar(T.zo[:], T.x143[:], T.gcol[:], None, ALU.is_equal))
+    vs("c_zc", 144, ["x143", "gcol", "wcol"], ["zc"],
+       lambda: vec.tensor_scalar(T.zc[:], T.x143[:], T.gcol[:], T.wcol[:], ALU.is_equal, ALU.mult))
+    vs("c_zp", 144, ["x143", "gcol"], ["zp"], lambda: vec.tensor_scalar(T.zp[:], T.x143[:], T.gcol[:], BIG, ALU.is_equal, ALU.mult))
+    vs("c_zn", 144, ["x143", "gcol"], ["zn"], lambda: vec.tensor_scalar(T.zn[:], T.x143[:], T.gcol[:], -BIG, ALU.is_equal, ALU.mult))
+    vs("c_idp", 128, ["x143", "pcol"], ["idp"], lambda: vec.tensor_scalar(T.idp[:], T.x143[:, 15:143], T.pcol[:], None, ALU.is_equal))
+    vs("c_idn", 128, ["x143", "pcol"], ["idn"],
+       lambda: vec.tensor_scalar(T.idn[:], T.x143[:, 15:143], T.pcol[:], -1.0, ALU.is_equal, ALU.mult))
+    vs("c_uc2", 48, ["uc1b", "uc1i", "rcol"], ["uc2"],
+       lambda: vec.tensor_scalar(T.uc2[:], T.uc1[:], 0.0, T.rcol[:], ALU.mult, ALU.add))
+    vs("c_b0", 1, ["thi"], ["b0"], lambda: vec.tensor_scalar(T.b0[:], T.thi[:], -1.0, -0.5, ALU.mult, ALU.add))
+    op("c_sum", "p", "mm", 64, ["am", "one"], ["pki"], lambda: pe.matmul(T.pki[:, 256:257], T.am[:], T.one[:], True, True))
+    vs("c_b1", 1, ["pki", "b0"], ["b1"], lambda: vec.tensor_scalar(T.b1[:], T.pki[:, 256:257], -256.0, T.b0[:], ALU.mult, ALU.add))
+
+    others = [c for c in T.cores if c != core]
+    near = [c for c in others if c in topo.cores_of(core)]
+    far = [c for c in others if c not in near]
+    fe = topo.engines(core, far[0])
+    eng = {}
+    for i, c in enumerate(far):
+        k = len(fe) // len(far)
+        eng[c] = fe[i * k:(i + 1) * k]
+    for c in near:
+        eng[c] = [e for e in topo.engines(core, c) if e not in fe]
+    total = sum(len(x) for x in eng.values())
+
+    def send(name, ap, rsem, lsem, reads, arrives, kind):
+        def fn():
+            trs = []
+            for c in far + near:
+                rid, pid = topo.addr(c, core)
+                trs.append(RemoteDMATransfer(dst_ids=[DstId(rid=rid, pnc=pid)], dma_engine_mask=sum(1 << e for e in eng[c]),
+                                             remote_sem=T.sem[rsem], src=ap, dst=ap))
+            return g.remote_dma_fused(trs, local_sem=T.sem[lsem])
+        op(name, "g", kind, total, reads, [arrives], fn, (rsem, lsem))
+
+    CH = [dict(blocks=[0], c0=0, k=32, bank="pkb", pw0=32 * rank, pwn=128, wn=M),
+          dict(blocks=[1, 2], c0=32, k=64, bank="pki", pw0=128, pwn=192, wn=M + V - B)]
+
+    def own(r, b):
+        if r == RO:
+            return T.fin[:, B * b:B * (b + 1)]
+        a = own0 if b == 0 else INN + B * (b - 1)
+        return W[r][:, a:a + B]
+
+    def pm(r, ci):
+        ch = CH[ci]
+        if r == RO:
+            return T.pfin[:, ch["c0"]:ch["c0"] + ch["k"]]
+        return PW[r][:, ch["pw0"]:ch["pw0"] + ch["k"]]
+
+    def wrap(name, ci, col, z, src, skey, first):
+        ch = CH[ci]
+        k, a = ch["k"], 16 * ch["c0"]
+        out = T[ch["bank"]][:, col:col + k]
+
+        def fn():
+            last = None
+            for r in range(16):
+                last = pe.matmul(out, T[z][:, 15 - r:143 - r], src[:, a + r:a + 16 * k:16], first and r == 0, r == 15)
+            return last
+        op(name, "p", "mm", 16 * 64, [z] + [(skey, b) for b in ch["blocks"]], [ch["bank"]], fn)
+        return out
+
+    def gather(name, out, win, off, reads, writes):
+        if name in cfg:
+            op(name, "v", "gat", B, reads, writes, lambda: vec.tensor_copy(out, win.indirect(off)))
+        else:
+            op(name, "a", "gat", B, reads, writes, lambda: act.activation(out, win.indirect(off), AF.Copy))
+
+    def ab(r, b):
+        return T[("ah%d" if "T7_%d_%d" % (r, b) in cfg else "ab%d") % b][:]
+
+    def halves(r, b):
+        out, bias, src = ab(r, b), (255.75 if r == 0 else -0.25 * 2 ** r), own(r, b)
+        if "T7_%d_%d" % (r, b) in cfg:
+            vs("T7_%d_%d" % (r, b), B // 2, [("w", r, b)], [("ab", b)],
+               lambda: vec.tensor_scalar(out, src, bias, None, ALU.add))
+        else:
+            op("T7_%d_%d" % (r, b), "a", "op", B, [("w", r, b)], [("ab", b)],
+               lambda: act.activation(out, src, AF.Copy, bias=bias))
+
+    def chunk_round(r, ci):
+        ch = CH[ci]
+        k, c0, bank, blocks = ch["k"], ch["c0"], ch["bank"], ch["blocks"]
+        t = "_%d_%d" % (r, ci)
+        cs = slice(c0, c0 + k)
+        p = pm(r, ci)
+        pk = ("pw", r, ci)
+        wkeys = [("w", r, 0), ("wr", r)] + ([("w", r, 1), ("w", r, 2)] if ci else [])
+        pkeys = [("pw", r, 0), ("pr", r)] + ([("pw", r, 1)] if ci else [])
+        ohk = ["oh0", "oh1", "oh2", "ohb"] + (["ohi"] if ci else [])
+        inv = 1.0 / 2 ** r
+        vs("up" + t, k, [pk], [("up", ci)], lambda: vec.tensor_scalar(T.up[:, cs], p, 1024.0, None, ALU.add))
+        vs("u4" + t, k, [pk], [("u4", ci)],
+           lambda: vec.tensor_scalar(T.u4[:, cs], p, 1.0 / 16, 64 - 15.0 / 32, ALU.mult, ALU.add))
+        for b in blocks:
+            halves(r, b)
+        for b in blocks:
+            bs, os_ = slice(B * b, B * (b + 1)), slice(32 * b, 32 * (b + 1))
+            gather("T8_%d_%d" % (r, b), T.msk[:, bs], T.oh[:, 0:ch["wn"]], T.up[:, os_], ohk + [("up", ci)], [("msk", b)])
+            op("T1_%d_%d" % (r, b), "v", "gat", B, pkeys + [("u4", ci), ("msk", b)], [("cand", b)],
+               lambda bs=bs, os_=os_: vec.tensor_tensor(T.cand[:, bs], PW[r][:, 0:ch["pwn"]].indirect(T.u4[:, os_]),
+                                                        T.msk[:, bs], ALU.mult))
+            op("sa_%d_%d" % (r, b), "p", "mm", B, ["am", ("w", r, b)], [("ps", b)],
+               lambda b=b: pe.matmul(T["ps%d" % b][:], T.am[:], own(r, b), True, False))
+            op("ea_%d_%d" % (r, b), "p", "mm", B, ["idp", ("w", r, b)], [("pe", b)],
+               lambda b=b: pe.matmul(T["pe%d" % b][:], T.idp[:], own(r, b), True, False))
+        hm = wrap("wh" + t, ci, 0, "zo", T.cand, "cand", True)
+        vs("uh" + t, k, [bank], [("uh", ci)], lambda: vec.tensor_scalar(T.uh[:, cs], hm, 1024.0, None, ALU.add))
+        vs("dh" + t, k, [bank, pk], [("dh", ci)], lambda: vec.tensor_tensor(T.dh[:, cs], hm, p, ALU.subtract))
+        bias = T.b0 if r == 0 else T.b1
+        for b in blocks:
+            bs, os_ = slice(B * b, B * (b + 1)), slice(32 * b, 32 * (b + 1))
+            gather("T2_%d_%d" % (r, b), T.dd[:, bs], W[r][:, OFF:OFF + ch["wn"]], T.uh[:, os_], wkeys + [("uh", ci)], [("dd", b)])
+            op("sd_%d_%d" % (r, b), "p", "mm", B, ["am", ("dd", b)], [("ps", b)],
+               lambda b=b, bs=bs: pe.matmul(T["ps%d" % b][:], T.am[:], T.dd[:, bs], False, True))
+            op("ed_%d_%d" % (r, b), "p", "mm", B, ["idn", ("dd", b)], [("pe", b)],
+               lambda b=b, bs=bs: pe.matmul(T["pe%d" % b][:], T.idn[:], T.dd[:, bs], False, True))
+            op("T3_%d_%d" % (r, b), "a", "op", B, [("ps", b), "b0", "b1"], [("sg", b)],
+               lambda b=b, bs=bs: act.activation(T.sg[:, bs], T["ps%d" % b][:], AF.Sign, bias=bias[:], scale=inv))
+            op("T4_%d_%d" % (r, b), "a", "op", B, [("pe", b)], [("ae", b)],
+               lambda b=b, bs=bs: act.activation(T.ae[:, bs], T["pe%d" % b][:], AF.Abs, scale=inv))
+        cd = wrap("wc" + t, ci, 64, "zc", T.sg, "sg", True)
+        vs("uc" + t, k, [bank], [("uc", ci)], lambda: vec.tensor_scalar(T.uc[:, cs], cd, 2047.5, None, ALU.add))
+        u = T[bank][:, 128:128 + k]
+
+        def consts():
+            pe.matmul(u, T.idp[:], T.uc1[:, cs], True, False)
+            return pe.matmul(u, T.idp[:], T.uc2[:, cs], False, False)
+        op("uk" + t, "p", "mm", 128, ["idp", "uc1b", "uc1i", "uc2"], [bank], consts)
+        for b in blocks:
+            bs, os_ = slice(B * b, B * (b + 1)), slice(32 * b, 32 * (b + 1))
+            op("T5_%d_%d" % (r, b), "v", "gat", B, ["clrs", ("uc", ci), ("ae", b)], [("viol", b)],
+               lambda bs=bs, os_=os_: vec.tensor_tensor(T.viol[:, bs], T.clrs[:].indirect(T.uc[:, os_]), T.ae[:, bs], ALU.is_lt))
+        wrap("wu" + t, ci, 128, "zn" if ci else "zp", T.viol, "viol", False)
+        vs("sl" + t, k, [bank, pk], [("sl", ci)], lambda: vec.tensor_tensor(T.sl[:, cs], u, p, ALU.max if ci else ALU.min))
+        vs("ok" + t, k, [bank], [("ok", ci)],
+           lambda: vec.tensor_scalar(T.okf[:, cs], u, 0.0 if ci else -1024.5, None, ALU.is_gt if ci else ALU.is_lt))
+        vs("us" + t, k, [("sl", ci)], [("us", ci)],
+           lambda: vec.tensor_scalar(T.us[:, cs], T.sl[:, cs], 1024.0 if ci else 1024.0 + OFF, None, ALU.add))
+        vs("tt" + t, 2 * k, [("ok", ci), ("dh", ci)], [("tt", ci)],
+           lambda: vec.tensor_tensor(T.tt[:, cs], T.okf[:, cs], T.dh[:, cs], ALU.mult))
+        vs("pn" + t, 2 * k, [("tt", ci), pk], [("pw", r + 1, ci)], lambda: vec.tensor_tensor(pm(r + 1, ci), T.tt[:, cs], p, ALU.add))
+        if ci == 0 and r + 1 < RO:
+            send("sp%d" % (r + 1), pm(r + 1, 0), "ap%d" % (r + 1), "lp%d" % (r + 1), [("pw", r + 1, 0)], ("pr", r + 1), "sendp")
+        win = W[r][:, OFF:WW] if ci else W[r][:, 0:INN]
+        for b in blocks:
+            os_ = slice(32 * b, 32 * (b + 1))
+            op("T6_%d_%d" % (r, b), "v", "gat", B, wkeys + [("wd", r, ci), ("us", ci), ("ab", b)], [("w", r + 1, b)],
+               lambda b=b, os_=os_: vec.tensor_tensor(own(r + 1, b), win.indirect(T.us[:, os_]), ab(r, b), ALU.add))
+        if r + 1 < RO:
+            if ci == 0:
+                send("sq%d" % (r + 1), own(r + 1, 0), "aq%d" % (r + 1), "lq%d" % (r + 1), [("w", r + 1, 0)], ("wr", r + 1), "sendq")
+                dma("db%d" % r, "s", W[r + 1][:, 0:B], own(r + 1, 0), [("w", r + 1, 0), ("wr", r + 1)], [("wd", r + 1, 0)],
+                    "db%d" % r, 300)
+            else:
+                dma("di%d" % r, "s", W[r + 1][:, DUP:WW], W[r + 1][:, INN:DUP], [("w", r + 1, 1), ("w", r + 1, 2)],
+                    [("wd", r + 1, 1)], "di%d" % r, 600)
+        else:
+            vs("yp" + t, k, [("pw", RO, ci)], [("yps", ci)], lambda: vec.tensor_scalar(T.yps[:, cs], pm(RO, ci), 1024.0, None, ALU.add))
+            dma("styp%d" % ci, "s", T.yp[:, cs], T.yps[:, cs], [("yps", ci)], [], "st%d" % (3 + ci), 0)
+            for b in blocks:
+                bs = slice(B * b, B * (b + 1))
+                if "fin%d" % b in cfg:
+                    vs("fin%d" % b, B // 2, [("w", RO, b)], [("yq", b)],
+                       lambda bs=bs: vec.tensor_scalar(T.yqs[:, bs], T.fin[:, bs], 1.0 / 2 ** RO, -128.0, ALU.mult, ALU.add))
+                else:
+                    op("fin%d" % b, "a", "op", B, [("w", RO, b)], [("yq", b)],
+                       lambda bs=bs: act.activation(T.yqs[:, bs], T.fin[:, bs], AF.Copy, bias=-128.0, scale=1.0 / 2 ** RO))
+                dma("styq%d" % b, "s", T.yq[:, bs], T.yqs[:, bs], [("yq", b)], [], "st%d" % b, 300)
+
+    vs("pm0", 32, ["pari"], [("pw", 0, 0)], lambda: vec.tensor_scalar(pm(0, 0), T.pari[:, 0:32], -1024.0, None, ALU.add))
+    send("sp0", pm(0, 0), "ap0", "lp0", [("pw", 0, 0)], ("pr", 0), "sendp")
+    send("sq0", own(0, 0), "aq0", "lq0", [("w", 0, 0)], ("wr", 0), "sendq")
+    vs("pm1", 64, ["pari"], [("pw", 0, 1)], lambda: vec.tensor_scalar(pm(0, 1), T.pari[:, 32:96], -1024.0, None, ALU.add))
+    for r in range(RO):
+        chunk_round(r, 0)
+        chunk_round(r, 1)
+
+    writer, readers = {}, {}
+    for i, o in enumerate(ops):
+        d = set()
+        for x in o["reads"]:
+            if x in writer:
+                d.add(writer[x])
+        for x in o["writes"]:
+            if x in writer:
+                d.add(writer[x])
+            d.update(readers.get(x, []))
+        d.discard(i)
+        o["deps"] = sorted(d)
+        for x in o["reads"]:
+            readers.setdefault(x, []).append(i)
+        for x in o["writes"]:
+            writer[x] = i
+            readers[x] = []
+    return ops
+
+
+def rank_program(g, core, T, topo):
+    rank = T.rank_of(core)
+    if rank is None:
+        return
+    ops = build_ops(g, T, topo, core, rank, CFG)
+    loads = [i for i, o in enumerate(ops) if o["name"].startswith("l_")]
+    order = loads + [i for i in ORDER if i not in loads]
+    queue = {"v": g.vector, "a": g.scalar, "p": g.tensor, "s": g.sync, "g": g}
+    esem = {"v": "sv", "a": "sa", "p": "sp", "g": "sgp"}
+    count, token, seen, ends = {}, {}, {}, {}
+    for i in order:
+        o = ops[i]
+        e = o["eng"]
+        need = {}
+        for d in o["deps"]:
+            if e == "p" and ops[d]["eng"] == "p":
+                continue
+            s, v = token[d]
+            need[s] = max(need.get(s, 0), v)
+        for s, v in need.items():
+            if seen.get((e, s), 0) < v:
+                queue[e].wait_ge(T.sem[s], v)
+                seen[(e, s)] = v
+        ins = o["fn"]()
+        if o["kind"] == "dma":
+            ins.then_inc(T.sem[o["sem"]], 16)
+            token[i] = (o["sem"], 16)
+        elif o["kind"] in ("sendp", "sendq"):
+            token[i] = (o["sem"][0], o["n"])
+            ends[o["sem"][1]] = o["n"]
+        else:
+            count[e] = count.get(e, 0) + 1
+            ins.then_inc(T.sem[esem[e]], 1)
+            token[i] = (esem[e], count[e])
+        ends[token[i][0]] = token[i][1]
+    for s, v in ends.items():
+        if not any(k[1] == s and x >= v for k, x in seen.items()):
+            g.wait_ge(T.sem[s], v)

@@ -18,8 +18,7 @@ for _n, _w, _d in [
     ("clrs", C, "bfloat16"), ("am", 128, "bfloat16"), ("thi", 1, "int32"), ("pari", 96, "int32"),
     ("oh", 3072, "bfloat16"), ("msk", V, "bfloat16"), ("cand", V, "float16"), ("dd", V, "bfloat16"),
     ("sg", V, "bfloat16"), ("ae", V, "bfloat16"), ("viol", V, "bfloat16"),
-    ("ab0", B, "float32"), ("ab1", B, "float32"), ("ab2", B, "float32"),
-    ("ah0", B, "float16"), ("ah1", B, "float16"), ("ah2", B, "float16"),
+    ("ab0", B, "float32"), ("ab2", B, "float32"), ("ah0", B, "float16"), ("ah2", B, "float16"),
     ("u4", 96, "uint16"), ("up", 96, "uint16"), ("uh", 96, "uint16"), ("uc", 96, "uint16"), ("us", 96, "uint16"),
     ("dh", 96, "float32"), ("sl", 96, "float32"), ("okf", 96, "float32"), ("tt", 96, "float32"),
     ("pci", 1, "int32"), ("rci", 1, "int32"), ("pcol", 1, "float32"), ("rcol", 1, "float32"), ("gcol", 1, "float32"),
@@ -34,12 +33,12 @@ for _n in ["ps0", "ps1", "ps2", "pe0", "pe1", "pe2", "pkb", "pki"]:
     SCRATCH[_n] = ("psum", [128, 512], "float32")
 
 LOADS = ["par", "qb", "clr", "qi", "am", "th", "qdb", "qdi"]
-SEMAPHORES = ["sv", "sa", "sp", "sgp"] + ["ld_" + x for x in LOADS] + ["st%d" % i for i in range(5)]
+SEMAPHORES = ["sv", "sa", "sp", "sgp"] + ["ld_" + x for x in LOADS] + ["st%d" % i for i in range(6)]
 for _r in range(RO):
     SEMAPHORES += ["ap%d" % _r, "aq%d" % _r, "lp%d" % _r, "lq%d" % _r, "db%d" % _r, "di%d" % _r]
 
-CFG = {"T2_2_1", "T2_4_2", "T7_0_2", "T7_2_0", "T7_3_0", "T8_0_0", "T8_2_0", "fin2"}
-ORDER = [8,9,10,1,3,5,0,6,7,2,4,13,17,18,14,21,22,38,41,16,15,19,26,33,72,43,11,39,40,12,23,71,42,27,20,28,24,31,32,45,35,46,25,75,44,79,73,47,48,36,81,82,78,49,80,50,29,51,76,37,52,53,54,83,55,56,57,30,34,74,84,58,60,85,86,91,77,59,87,61,92,93,88,89,94,63,62,65,64,66,68,67,69,96,90,111,110,97,95,112,113,99,100,114,98,101,115,117,116,103,102,105,104,106,118,139,107,108,140,119,120,143,121,122,123,125,124,144,70,109,147,126,128,148,127,129,151,149,146,131,130,133,142,141,134,132,152,136,153,180,178,179,181,135,137,159,154,160,150,161,145,155,184,156,183,162,157,163,158,182,164,185,165,168,186,167,166,169,188,187,171,170,173,174,172,207,175,208,189,191,211,193,213,190,215,192,194,212,216,176,219,217,218,195,220,196,222,197,138,177,209,227,199,201,202,198,221,200,246,204,203,228,223,214,224,229,205,230,225,226,231,210,249,232,233,247,235,236,250,234,251,252,237,253,239,241,238,242,275,254,276,240,255,243,279,283,280,284,244,281,256,257,258,287,206,245,288,259,260,261,290,262,264,248,289,285,282,263,291,265,295,267,266,269,268,270,296,271,293,298,286,292,300,297,272,314,301,273,294,277,299,317,278,303,304,315,302,305,319,307,306,309,308,310,345,344,318,311,352,348,321,322,353,349,312,324,313,274,350,351,320,326,325,356,327,328,357,323,364,359,355,329,354,365,360,367,362,330,332,358,361,331,333,369,366,335,334,337,336,338,370,363,368,316,346,347,371,372,373,339,374,375,340,377,376,380,381,378,386,379,382,342,384,343,341,385,387,383]
+CFG = {"P6_0_1", "T2_4_2", "T7_1_2", "T7_3_2", "fin1"}
+ORDER = [0,7,6,4,2,9,12,8,11,10,19,38,41,14,17,32,13,15,16,18,21,26,22,71,23,20,42,100,99,33,34,39,1,44,5,3,24,72,30,27,28,101,25,43,45,102,73,46,40,103,53,81,75,48,104,105,47,36,49,51,74,35,50,107,37,29,31,52,55,54,76,56,57,78,77,106,58,60,79,110,59,80,61,108,83,63,62,65,64,66,82,109,85,111,84,112,113,67,68,86,126,88,128,129,69,87,114,115,117,95,89,116,131,118,91,93,90,94,155,92,120,127,122,156,123,130,184,183,157,96,186,158,132,97,137,160,133,119,134,98,187,121,161,162,124,135,136,138,189,139,70,125,141,140,142,190,144,185,163,192,159,188,194,143,145,164,165,167,147,146,149,148,150,152,166,193,169,151,168,196,153,191,170,210,195,171,198,172,199,197,212,213,201,173,200,174,176,175,211,177,178,239,214,180,241,202,179,181,216,204,203,240,206,205,207,182,267,268,217,208,218,242,219,270,215,249,221,272,220,222,244,271,245,154,209,223,224,225,273,247,226,246,228,274,275,227,243,248,229,278,250,276,251,231,230,233,232,234,236,235,277,253,279,252,280,281,237,282,295,254,256,294,283,285,296,297,269,255,299,257,284,305,263,286,258,259,261,260,262,323,298,288,290,324,291,351,287,352,264,325,300,265,354,302,301,326,303,266,328,304,306,289,355,292,293,238,307,308,357,309,358,359,330,310,329,312,353,360,331,362,327,356,361,311,313,332,333,364,335,315,314,317,316,318,320,319,334,321,337,363,366,378,338,336,380,365,381,340,367,369,347,339,341,368,383,370,342,344,343,345,346,379,408,382,348,410,349,384,389,350,372,371,374,373,409,375,440,385,411,376,387,443,412,418,413,388,445,390,414,441,386,444,415,322,377,391,392,393,446,416,394,396,395,417,419,397,420,421,447,448,449,398,451,450,422,452,453,454,399,400,403,423,425,455,424,456,458,426,457,459,432,427,406,442,429,428,401,430,433,434,435,431,402,436,460,462,465,404,461,438,463,464,466,468,407,405,437,439,469,467]
 
 
 def build_ops(g, T, topo, core, rank, cfg):
@@ -59,7 +58,7 @@ def build_ops(g, T, topo, core, rank, cfg):
 
     dma("l_par", "s", T.pari[:], T.par[:], [], ["pari"], "ld_par", 0)
     dma("l_qb", "a", W[0][:, own0:own0 + B], T.q[:, 0:B], [], [("w", 0, 0)], "ld_qb", 300)
-    dma("l_qi", "s", W[0][:, INN:DUP], T.q[:, B:V], ["ld1"], [("w", 0, 1), ("w", 0, 2)], "ld_qi", 900)
+    dma("l_qi", "s", W[0][:, INN:DUP], T.q[:, B:V], [], [("w", 0, 1), ("w", 0, 2)], "ld_qi", 900)
     dma("l_am", "a", T.am[:], T.amat[:], [], ["am"], "ld_am", 500)
     dma("l_clr", "s", T.clrs[:], T.clr[:], [], ["clrs"], "ld_clr", 4000)
     dma("l_th", "a", T.thi[:], T.th[:], [], ["thi"], "ld_th", 600)
@@ -131,7 +130,9 @@ def build_ops(g, T, topo, core, rank, cfg):
         op(name, "g", kind, total, reads, [arrives], fn, (rsem, lsem))
 
     CH = [dict(blocks=[0], c0=0, k=32, bank="pkb", pw0=32 * rank, pwn=128, wn=M),
-          dict(blocks=[1, 2], c0=32, k=64, bank="pki", pw0=128, pwn=192, wn=M + V - B)]
+          dict(blocks=[1], c0=32, k=32, bank="pki", pw0=128, pwn=192, wn=M + V - B),
+          dict(blocks=[2], c0=64, k=32, bank="pe2", pw0=160, pwn=192, wn=M + V - B)]
+    EB = [0, 1, 0]
 
     def own(r, b):
         if r == RO:
@@ -184,14 +185,15 @@ def build_ops(g, T, topo, core, rank, cfg):
         p = pm(r, ci)
         pk = ("pw", r, ci)
         wkeys = [("w", r, 0), ("wr", r)] + ([("w", r, 1), ("w", r, 2)] if ci else [])
-        pkeys = [("pw", r, 0), ("pr", r)] + ([("pw", r, 1)] if ci else [])
+        pkeys = [("pw", r, 0), ("pr", r)] + ([("pw", r, 1), ("pw", r, 2)] if ci else [])
         ohk = ["oh0", "oh1", "oh2", "ohb"] + (["ohi"] if ci else [])
         inv = 1.0 / 2 ** r
         vs("up" + t, k, [pk], [("up", ci)], lambda: vec.tensor_scalar(T.up[:, cs], p, 1024.0, None, ALU.add))
         vs("u4" + t, k, [pk], [("u4", ci)],
            lambda: vec.tensor_scalar(T.u4[:, cs], p, 1.0 / 16, 64 - 15.0 / 32, ALU.mult, ALU.add))
         for b in blocks:
-            halves(r, b)
+            if b != 1:
+                halves(r, b)
         for b in blocks:
             bs, os_ = slice(B * b, B * (b + 1)), slice(32 * b, 32 * (b + 1))
             gather("T8_%d_%d" % (r, b), T.msk[:, bs], T.oh[:, 0:ch["wn"]], T.up[:, os_], ohk + [("up", ci)], [("msk", b)])
@@ -200,8 +202,6 @@ def build_ops(g, T, topo, core, rank, cfg):
                                                         T.msk[:, bs], ALU.mult))
             op("sa_%d_%d" % (r, b), "p", "mm", B, ["am", ("w", r, b)], [("ps", b)],
                lambda b=b: pe.matmul(T["ps%d" % b][:], T.am[:], own(r, b), True, False))
-            op("ea_%d_%d" % (r, b), "p", "mm", B, ["idp", ("w", r, b)], [("pe", b)],
-               lambda b=b: pe.matmul(T["pe%d" % b][:], T.idp[:], own(r, b), True, False))
         hm = wrap("wh" + t, ci, 0, "zo", T.cand, "cand", True)
         vs("uh" + t, k, [bank], [("uh", ci)], lambda: vec.tensor_scalar(T.uh[:, cs], hm, 1024.0, None, ALU.add))
         vs("dh" + t, k, [bank, pk], [("dh", ci)], lambda: vec.tensor_tensor(T.dh[:, cs], hm, p, ALU.subtract))
@@ -211,12 +211,15 @@ def build_ops(g, T, topo, core, rank, cfg):
             gather("T2_%d_%d" % (r, b), T.dd[:, bs], W[r][:, OFF:OFF + ch["wn"]], T.uh[:, os_], wkeys + [("uh", ci)], [("dd", b)])
             op("sd_%d_%d" % (r, b), "p", "mm", B, ["am", ("dd", b)], [("ps", b)],
                lambda b=b, bs=bs: pe.matmul(T["ps%d" % b][:], T.am[:], T.dd[:, bs], False, True))
-            op("ed_%d_%d" % (r, b), "p", "mm", B, ["idn", ("dd", b)], [("pe", b)],
-               lambda b=b, bs=bs: pe.matmul(T["pe%d" % b][:], T.idn[:], T.dd[:, bs], False, True))
+            eb = T["pe%d" % EB[b]][:]
+            op("ea_%d_%d" % (r, b), "p", "mm", B, ["idp", ("w", r, b)], [("pe", EB[b])],
+               lambda b=b, eb=eb: pe.matmul(eb, T.idp[:], own(r, b), True, False))
+            op("ed_%d_%d" % (r, b), "p", "mm", B, ["idn", ("dd", b)], [("pe", EB[b])],
+               lambda bs=bs, eb=eb: pe.matmul(eb, T.idn[:], T.dd[:, bs], False, True))
             op("T3_%d_%d" % (r, b), "a", "op", B, [("ps", b), "b0", "b1"], [("sg", b)],
                lambda b=b, bs=bs: act.activation(T.sg[:, bs], T["ps%d" % b][:], AF.Sign, bias=bias[:], scale=inv))
-            op("T4_%d_%d" % (r, b), "a", "op", B, [("pe", b)], [("ae", b)],
-               lambda b=b, bs=bs: act.activation(T.ae[:, bs], T["pe%d" % b][:], AF.Abs, scale=inv))
+            op("T4_%d_%d" % (r, b), "a", "op", B, [("pe", EB[b])], [("ae", b)],
+               lambda eb=eb, bs=bs: act.activation(T.ae[:, bs], eb, AF.Abs, scale=inv))
         cd = wrap("wc" + t, ci, 64, "zc", T.sg, "sg", True)
         vs("uc" + t, k, [bank], [("uc", ci)], lambda: vec.tensor_scalar(T.uc[:, cs], cd, 2047.5, None, ALU.add))
         u = T[bank][:, 128:128 + k]
@@ -243,14 +246,28 @@ def build_ops(g, T, topo, core, rank, cfg):
         win = W[r][:, OFF:WW] if ci else W[r][:, 0:INN]
         for b in blocks:
             os_ = slice(32 * b, 32 * (b + 1))
-            op("T6_%d_%d" % (r, b), "v", "gat", B, wkeys + [("wd", r, ci), ("us", ci), ("ab", b)], [("w", r + 1, b)],
+            if b == 1:
+                bs, q, bi = slice(B * b, B * (b + 1)), T["pe%d" % b][:], (255.75 if r == 0 else -0.25 * 2 ** r)
+                op("ma_%d_%d" % (r, b), "p", "mm", B, ["idp", ("w", r, b)], [("pe", b)],
+                   lambda b=b, q=q: pe.matmul(q, T.idp[:], own(r, b), True, False))
+                gather("G6_%d_%d" % (r, b), T.dd[:, bs], win, T.us[:, os_], wkeys + [("wd", r, ci), ("us", ci)], [("dd", b)])
+                op("mb_%d_%d" % (r, b), "p", "mm", B, ["idp", ("dd", b)], [("pe", b)],
+                   lambda bs=bs, q=q: pe.matmul(q, T.idp[:], T.dd[:, bs], False, True))
+                if "P6_%d_%d" % (r, b) in cfg:
+                    vs("P6_%d_%d" % (r, b), B, [("pe", b)], [("w", r + 1, b)],
+                       lambda b=b, q=q, bi=bi: vec.tensor_scalar(own(r + 1, b), q, bi, None, ALU.add))
+                else:
+                    op("P6_%d_%d" % (r, b), "a", "op", B, [("pe", b)], [("w", r + 1, b)],
+                       lambda b=b, q=q, bi=bi: act.activation(own(r + 1, b), q, AF.Copy, bias=bi))
+                continue
+            op("T6_%d_%d" % (r, b), "v", "gat", B, wkeys + [("wd", r, min(ci, 1)), ("us", ci), ("ab", b)], [("w", r + 1, b)],
                lambda b=b, os_=os_: vec.tensor_tensor(own(r + 1, b), win.indirect(T.us[:, os_]), ab(r, b), ALU.add))
         if r + 1 < RO:
             if ci == 0:
                 send("sq%d" % (r + 1), own(r + 1, 0), "aq%d" % (r + 1), "lq%d" % (r + 1), [("w", r + 1, 0)], ("wr", r + 1), "sendq")
                 dma("db%d" % r, "s", W[r + 1][:, 0:B], own(r + 1, 0), [("w", r + 1, 0), ("wr", r + 1)], [("wd", r + 1, 0)],
                     "db%d" % r, 300)
-            else:
+            elif ci == 2:
                 dma("di%d" % r, "s", W[r + 1][:, DUP:WW], W[r + 1][:, INN:DUP], [("w", r + 1, 1), ("w", r + 1, 2)],
                     [("wd", r + 1, 1)], "di%d" % r, 600)
         else:
@@ -269,10 +286,11 @@ def build_ops(g, T, topo, core, rank, cfg):
     vs("pm0", 32, ["pari"], [("pw", 0, 0)], lambda: vec.tensor_scalar(pm(0, 0), T.pari[:, 0:32], -1024.0, None, ALU.add))
     send("sp0", pm(0, 0), "ap0", "lp0", [("pw", 0, 0)], ("pr", 0), "sendp")
     send("sq0", own(0, 0), "aq0", "lq0", [("w", 0, 0)], ("wr", 0), "sendq")
-    vs("pm1", 64, ["pari"], [("pw", 0, 1)], lambda: vec.tensor_scalar(pm(0, 1), T.pari[:, 32:96], -1024.0, None, ALU.add))
+    vs("pm1", 64, ["pari"], [("pw", 0, 1), ("pw", 0, 2)],
+       lambda: vec.tensor_scalar(PW[0][:, 128:192], T.pari[:, 32:96], -1024.0, None, ALU.add))
     for r in range(RO):
-        chunk_round(r, 0)
-        chunk_round(r, 1)
+        for ci in range(3):
+            chunk_round(r, ci)
 
     writer, readers = {}, {}
     for i, o in enumerate(ops):

@@ -7,105 +7,127 @@ OFF = B
 INN = OFF + M
 DUP = INN + V - B
 WW = DUP + V - B
-BIG = 8192.0
+NAMES = M + V - B
+LW = NAMES // 16
+CEN = NAMES // 2
+PK = 4096.0
+MID = PK / 2
+BIG = 2.0 ** 24
+SNAP = 1.5 * 2.0 ** 35
 
 SCRATCH = {}
 for _r in range(RO):
     SCRATCH["w%d" % _r] = ("sbuf", [128, WW], "bfloat16")
-    SCRATCH["pw%d" % _r] = ("sbuf", [128, 192], "float32")
+    SCRATCH["pw%d" % _r] = ("sbuf", [128, LW], "float32")
 for _n, _w, _d in [
     ("fin", V, "bfloat16"), ("yqs", V, "bfloat16"), ("pfin", 96, "float32"), ("yps", 96, "float32"),
-    ("clrs", C, "bfloat16"), ("am", 128, "bfloat16"), ("thi", 1, "int32"), ("pari", 96, "int32"),
-    ("oh", 3072, "bfloat16"), ("msk", V, "bfloat16"), ("cand", V, "float16"), ("dd", V, "bfloat16"),
-    ("sg", V, "bfloat16"), ("ae", V, "bfloat16"), ("viol", V, "bfloat16"),
-    ("ab0", B, "float32"), ("ab2", B, "float32"), ("ah0", B, "float16"), ("ah2", B, "float16"),
+    ("clrs", C, "bfloat16"), ("am", 128, "bfloat16"), ("am2", 128, "bfloat16"), ("thi", 1, "int32"), ("pari", 96, "int32"),
+    ("oh", NAMES, "bfloat16"), ("nr", NAMES, "float32"), ("msk", V, "bfloat16"), ("cand", V, "float16"), ("dd", V, "bfloat16"),
+    ("gg", V, "bfloat16"), ("aa", V, "bfloat16"), ("sg", V, "bfloat16"), ("ae", V, "bfloat16"), ("viol", V, "bfloat16"),
+    ("ab", V, "float32"), ("ah", V, "float16"),
     ("u4", 96, "uint16"), ("up", 96, "uint16"), ("uh", 96, "uint16"), ("uc", 96, "uint16"), ("us", 96, "uint16"),
-    ("dh", 96, "float32"), ("sl", 96, "float32"), ("okf", 96, "float32"), ("tt", 96, "float32"),
+    ("un", 96, "uint16"), ("h4", 96, "float16"),
+    ("keep", 96, "float32"), ("hs", 96, "float16"), ("sl", 96, "float32"), ("tt", 96, "float32"),
     ("pci", 1, "int32"), ("rci", 1, "int32"), ("pcol", 1, "float32"), ("rcol", 1, "float32"), ("gcol", 1, "float32"),
-    ("wcol", 1, "float32"), ("b0", 1, "float32"), ("b1", 1, "float32"), ("one", 1, "bfloat16"),
+    ("wcol", 1, "float32"), ("b0", 1, "float32"), ("b1", 1, "float32"), ("nth", 8, "float32"), ("half", 96, "bfloat16"),
+    ("one", 1, "bfloat16"),
     ("x143", 144, "float32"), ("x16", 256, "bfloat16"), ("two", 16, "float32"), ("zero", 16, "float32"),
     ("pk2", 16, "float32"), ("pk3", 16, "float32"),
     ("zc", 144, "bfloat16"), ("zo", 144, "float16"), ("zp", 144, "bfloat16"), ("zn", 144, "bfloat16"),
-    ("idp", 128, "bfloat16"), ("idn", 128, "bfloat16"), ("uc1", 96, "bfloat16"), ("uc2", 96, "bfloat16"),
+    ("idp", 128, "bfloat16"), ("idn", 128, "bfloat16"), ("idk", 128, "float16"), ("uc1", 96, "bfloat16"), ("uc2", 96, "float16"),
+    ("idw", 128, "float32"), ("idm", 128, "float16"), ("idh", 128, "float16"),
 ]:
     SCRATCH[_n] = ("sbuf", [128, _w], _d)
-for _n in ["ps0", "ps1", "ps2", "pe0", "pe1", "pe2", "pkb", "pki"]:
-    SCRATCH[_n] = ("psum", [128, 512], "float32")
+for _n in range(8):
+    SCRATCH["bank%d" % _n] = ("psum", [128, 512], "float32")
 
-LOADS = ["par", "qb", "clr", "qi", "am", "th", "qdb", "qdi"]
-SEMAPHORES = ["sv", "sa", "sp", "sgp"] + ["ld_" + x for x in LOADS] + ["st%d" % i for i in range(6)]
+LOADS = ["par", "qb", "clr", "clr2", "qi", "am", "th", "qdb", "qdi"]
+SEMAPHORES = ["sv", "sa", "sp", "sgp"] + ["ld_" + x for x in LOADS] + ["st%d" % i for i in range(16)]
 for _r in range(RO):
-    SEMAPHORES += ["ap%d" % _r, "aq%d" % _r, "lp%d" % _r, "lq%d" % _r, "db%d" % _r, "di%d" % _r]
+    SEMAPHORES += [x + "%d" % _r for x in ["ap", "lp", "db", "di", "nr"]]
+    SEMAPHORES += [x + "%d_%d" % (_r, j) for x in ["aq", "lq"] for j in range(2)]
 
-CFG = {"P6_0_1", "T2_4_2", "T7_1_2", "T7_3_2", "fin1"}
-ORDER = [0,7,6,4,2,9,12,8,11,10,19,38,41,14,17,32,13,15,16,18,21,26,22,71,23,20,42,100,99,33,34,39,1,44,5,3,24,72,30,27,28,101,25,43,45,102,73,46,40,103,53,81,75,48,104,105,47,36,49,51,74,35,50,107,37,29,31,52,55,54,76,56,57,78,77,106,58,60,79,110,59,80,61,108,83,63,62,65,64,66,82,109,85,111,84,112,113,67,68,86,126,88,128,129,69,87,114,115,117,95,89,116,131,118,91,93,90,94,155,92,120,127,122,156,123,130,184,183,157,96,186,158,132,97,137,160,133,119,134,98,187,121,161,162,124,135,136,138,189,139,70,125,141,140,142,190,144,185,163,192,159,188,194,143,145,164,165,167,147,146,149,148,150,152,166,193,169,151,168,196,153,191,170,210,195,171,198,172,199,197,212,213,201,173,200,174,176,175,211,177,178,239,214,180,241,202,179,181,216,204,203,240,206,205,207,182,267,268,217,208,218,242,219,270,215,249,221,272,220,222,244,271,245,154,209,223,224,225,273,247,226,246,228,274,275,227,243,248,229,278,250,276,251,231,230,233,232,234,236,235,277,253,279,252,280,281,237,282,295,254,256,294,283,285,296,297,269,255,299,257,284,305,263,286,258,259,261,260,262,323,298,288,290,324,291,351,287,352,264,325,300,265,354,302,301,326,303,266,328,304,306,289,355,292,293,238,307,308,357,309,358,359,330,310,329,312,353,360,331,362,327,356,361,311,313,332,333,364,335,315,314,317,316,318,320,319,334,321,337,363,366,378,338,336,380,365,381,340,367,369,347,339,341,368,383,370,342,344,343,345,346,379,408,382,348,410,349,384,389,350,372,371,374,373,409,375,440,385,411,376,387,443,412,418,413,388,445,390,414,441,386,444,415,322,377,391,392,393,446,416,394,396,395,417,419,397,420,421,447,448,449,398,451,450,422,452,453,454,399,400,403,423,425,455,424,456,458,426,457,459,432,427,406,442,429,428,401,430,433,434,435,431,402,436,460,462,465,404,461,438,463,464,466,468,407,405,437,439,469,467]
+WHO = dict(names="mask", T8="a", T1="v", T2="a", T3="a", T5="v", upd="T", T7="v", G6="a", P6="a", fin="v")
+CFG = dict(chunks=[dict(WHO, c0=0, k=32, ps=[(0, 0), (6, 256)], pe=[(3, 0), (3, 256)], ls=(6, 0), T2="ae", T3="av", T7="a"),
+                   dict(WHO, c0=32, k=32, ps=[(1, 0)], pu=[(1, 0)], pe=[(4, 0)], ls=(7, 0), upd="G", names="rows", T1="a"),
+                   dict(WHO, c0=64, k=32, ps=[(2, 0)], pe=[(3, 0)], ls=(5, 0), names="rows")],
+           merge=("kp", "un", "wh"), near=1, stq="s", kp="v", lc=True,
+           late=dict(qi=[("pr", 0)], qdb=[("wr", 0, 0)], qdi=[("wr", 0, 0)]))
+ORDER = """
+T5.0@4+3 c_n0+2 sl.0@0+3 un.1@0+2 tt.0@0+3 us.0@0+3 pn.0@0+3 c_half01+2 kp.1+3 T7.2+3 tt.1@4+4 hc.1+3 ed.1@0+3
+sa.1@4+3 sl.0+3 c_half00+1 sd.1+3 ea.1+3 ed.1+3 ea.1@4+3 ea.2+3 ma.1@4+4 ea.2@4+3 sd.1@4+3 wu.0@4+3 ed.1@4+3 sd.2@0+3
+sd.2+3 wc.1@0+3 sd.2@4+3 mb.1@4+4 ea.2@0+3 T3.1+3 l_am+1 T4.1@0+3 T4.1+3 T3.2+3 c_nr1+1 wc.1+3 T3.1@4+3 T3.2@0+3
+wc.1@4+3 ed.2@4+3 ed.2+3 ed.2@0+3 T4.2@0+3 c_sum+2 wc.2+3 ea.0@0+2 wc.2@0+3 nr@0+2 styp0+5 di+4 sp_0+1 l_qi+2 sq_0_0+1
+l_clr2+1 di@0+4 kp.1@0+1 sp@0+3 sl.2@4+4 tt.0+3 pn.1@4+4 T6.0@0+3 c_wcol+2 kp.0@0+1 uc.1@0+3 us.0+3 us.2@4+4 pn.0+3
+T6.0+3 c_zc+2 c_oh1+1 sl.0@4+3 up.0@4+2 c_b1+2 bcp.0@4+2 c_idm+1 c_nr0 c_zero us.0@4+3 uc.1+3 c_zn+2 up.0+2 c_zp+2
+c_oh2+1 T5.1@0+3 uc.2@0+3 u4.0+2 T5.1+3 c_idw+1 c_oh3+1 c_pk2+1 c_gcol+1 l_clr+2 l_par i_p l_qdb+2 sp+3 sq.0@0+3
+styp1+5 i_u1+2 styp2+5 styq1+5 T4.2+3 sq.0+3 T4.1@4+3 T3.2@4+3 T8.0@4+2 T8.0+2 T8.0@0+1 P6.1@4+4 pn.0@4+4 uc.2+3
+T5.2@0+3 u4.0@4+2 T5.2+3 c_pcol T1.0+2 T1.0@4+2 ma.1+3 uk.1@0+3 uk.2+3 uk.2@0+3 wu.1@0+3 wu.2@0+3 tt.2@4+4 ea.0@4+2
+uk.1+3 wh.0@0+2 wu.1+3 sl.1+3 wu.2+3 sa.0@4+2 c_two wh.0@4+2 wh.0+2 wc.2@4+3 T6.2@4+4 pn.2@4+4 uh.0@0+2 c_rci sl.2+3
+tt.1+3 pm0 c_idn+1 sl.1@0+3 sl.2@0+3 tt.2+3 c_b0+1 hc.0@0+2 c_n1+2 T6.0@4+3 uc.1@4+3 us.1+3 c_idk+1 tt.1@0+3 fin1+4
+pn.1+3 pn.2+3 bT2.0@0+2 tt.2@0+3 T1.2@0+2 fin2+4 us.2+3 us.2@0+3 T5.1@4+3 uc.2@4+3 h4.1@4+2 uh.0@4+2 us.1@0+3 pn.1@0+3
+c_rcol c_pk3+1 pn.2@0+3 bcp.0+2 hc.0@4+2 h4.1+2 T7.2@0+2 c_am2+1 uh.0+2 styq2+5 i_u2+1 nr+2 styq0+4 nr@4+2 l_qdi+2
+db@0+3 i_16 i_143 T7.0@4+2 db+3 T7.0+2 G6.1@0+3 T4.2@4+3 G6.1+3 T7.0@0+1 T2.0@0+2 T2.0@4+2 uk.1@4+3 nm.1@4+2 nm.1+2
+sa.0@0+2 c_idh+1 hc.0+2 T6.2@0+3 bT2.0@4+2 un.1@4+2 T6.2+3 bT2.0+2 c_idp T5.2@4+3 ea.0+2 bsa.0@4+2 sd.0@4+2 bsa.0@0+2
+ed.0@0+2 bT4.0@4+2 l_qb sd.0@0+2 T1.1@0+2 sa.0+2 ma.1@0+3 T2.0+2 ed.0@4+2 bsd.0@4+2 bsa.0+2 mb.1+3 sd.0+2 ed.0+2
+bsd.0+2 bsd.0@0+2 wu.1@4+3 sa.2@4+2 sa.2+2 wh.1@0+2 sl.1@4+3 bT3.0@4+2 bT3.0@0+2 T1.2@4+2 tt.0@4+3 T7.2@4+2 us.1@4+3
+uh.1@0+2 c_one+1 c_zo+1 un.1+2 bcp.0@0 c_oh0 kp.0@4+2 kp.0+2 c_uc2+2 pm1 bT3.0+2 T3.0+2 T3.0@0+2 bT4.0+2 T4.0+2 T1.1+2
+G6.1@4+3 bT4.0@0+2 T3.0@4+2 wc.0@0+2 sa.1@0+2 uk.2@4+3 sa.2@0+2 wc.0+2 wc.0@4+2 uk.0+2 mb.1@0+3 P6.1@0+3 T1.1@4+2
+T4.0@0+2 T2.1@0+2 l_th P6.1+3 h4.1@0+1 hc.1@0+2 fin0+3 T1.0@0+1 uk.0@0+2 wh.1@4+2 nm.1@0+1 wu.2@4+3 T1.2+2 uc.0@4+2
+uc.0+2 u4.0@0 uc.0@0+2 wh.1+2 uk.0@4+2 ea.1@0+2 sd.1@0+2 kp.1@4+2 T5.0+2 uh.1+2 uh.1@4+2 up.0@0 T5.0@0+2 hc.1@4+2
+wu.0+2 T4.0@4+2 T2.1@4+2 wu.0@0+2 sa.1+2 T2.2@4+2 T2.2@0+2 T3.1@0+2 T2.1+2 T2.2+2
+"""
 
 
 def build_ops(g, T, topo, core, rank, cfg):
     ops = []
 
-    def op(name, eng, kind, n, reads, writes, fn, sem=None):
-        ops.append(dict(name=name, eng=eng, kind=kind, n=n, reads=reads, writes=writes, fn=fn, sem=sem))
+    def op(name, eng, kind, reads, writes, fn, sem=None, banks=()):
+        ops.append(dict(name=name, eng=eng, kind=kind, reads=reads, writes=writes, fn=fn, sem=sem, banks=banks))
 
     vec, act, pe = g.vector, g.scalar, g.tensor
     W = [T["w%d" % r] for r in range(RO)]
     PW = [T["pw%d" % r] for r in range(RO)]
     own0 = OFF + B * rank
+    CH = cfg["chunks"]
+    BORDER = [i for i, ch in enumerate(CH) if ch["c0"] < 32]
+    INNER = [i for i, ch in enumerate(CH) if ch["c0"] >= 32]
+    rows = any(ch["names"] == "rows" for ch in CH)
+    maski = any(CH[i]["names"] == "mask" for i in INNER)
 
-    def dma(name, eng, out, in_, reads, writes, sem, n):
+    def dma(name, eng, out, in_, reads, writes, sem):
         q = g.sync if eng == "s" else g.scalar
-        op(name, eng, "dma", n, reads, writes, lambda: q.dma_start(out, in_), sem)
+        op(name, eng, "dma", reads, writes, lambda: q.dma_start(out, in_), sem)
 
-    dma("l_par", "s", T.pari[:], T.par[:], [], ["pari"], "ld_par", 0)
-    dma("l_qb", "a", W[0][:, own0:own0 + B], T.q[:, 0:B], [], [("w", 0, 0)], "ld_qb", 300)
-    dma("l_qi", "s", W[0][:, INN:DUP], T.q[:, B:V], [], [("w", 0, 1), ("w", 0, 2)], "ld_qi", 900)
-    dma("l_am", "a", T.am[:], T.amat[:], [], ["am"], "ld_am", 500)
-    dma("l_clr", "s", T.clrs[:], T.clr[:], [], ["clrs"], "ld_clr", 4000)
-    dma("l_th", "a", T.thi[:], T.th[:], [], ["thi"], "ld_th", 600)
-    dma("l_qdb", "s", W[0][:, 0:B], T.q[:, 0:B], [], [("wd", 0, 0)], "ld_qdb", 4500)
-    dma("l_qdi", "s", W[0][:, DUP:WW], T.q[:, B:V], [], [("wd", 0, 1)], "ld_qdi", 5000)
+    def load(name, eng, out, in_, writes):
+        dma("l_" + name, eng, out, in_, cfg["late"].get(name, []), writes, "ld_" + name)
 
-    def gp(name, n, w, fn):
-        op(name, "g", "iota", n, [], [w], fn)
+    def gp(name, w, fn):
+        op(name, "g", "iota", [], [w], fn)
 
-    def vs(name, n, reads, writes, fn):
-        op(name, "v", "op", n, reads, writes, fn)
+    def vs(name, reads, writes, fn, banks=()):
+        op(name, "v", "op", reads, writes, fn, None, banks)
 
-    gp("i_p", 1, "pci", lambda: g.iota(T.pci[:], [[0, 1]], 0, 1))
-    gp("i_16", 256, "x16", lambda: g.iota(T.x16[:], [[0, 16], [1, 16]], 0, 0, allow_small_or_imprecise_dtypes=True))
-    gp("i_143", 144, "x143", lambda: g.iota(T.x143[:], [[1, 144]], -15, 0, allow_small_or_imprecise_dtypes=True))
-    gp("i_u1", 32, "uc1b", lambda: g.iota(T.uc1[:, 0:32], [[16, 32]], -OFF - 1024, 0, allow_small_or_imprecise_dtypes=True))
-    gp("i_u2", 64, "uc1i", lambda: g.iota(T.uc1[:, 32:96], [[16, 64]], DUP - OFF - 1024, 0, allow_small_or_imprecise_dtypes=True))
-    vs("c_two", 16, [], ["two"], lambda: vec.memset(T.two[:], 2.0))
-    vs("c_zero", 16, [], ["zero"], lambda: vec.memset(T.zero[:], 0.0))
-    vs("c_one", 1, [], ["one"], lambda: vec.memset(T.one[:], 1.0))
-    vs("c_pk2", 16, ["two", "zero"], ["pk2"],
-       lambda: vec.tensor_tensor_scan(T.pk2[:], T.two[:], T.zero[:], 0.25, ALU.mult, ALU.add))
-    vs("c_rci", 1, ["pci"], ["rci"], lambda: vec.tensor_scalar(T.rci[:], T.pci[:], 15, None, ALU.bitwise_and))
-    vs("c_rcol", 1, ["rci"], ["rcol"], lambda: vec.tensor_copy(T.rcol[:], T.rci[:]))
-    vs("c_pcol", 1, ["pci"], ["pcol"], lambda: vec.tensor_copy(T.pcol[:], T.pci[:]))
-    vs("c_gcol", 1, ["pcol", "rcol"], ["gcol"], lambda: vec.tensor_tensor(T.gcol[:], T.pcol[:], T.rcol[:], ALU.subtract))
-    vs("c_oh0", 128, ["x16", "rcol"], ["oh0"], lambda: vec.tensor_scalar(T.oh[:, 0:256], T.x16[:], T.rcol[:], None, ALU.is_equal))
-    vs("c_oh1", 128, ["oh0"], ["oh1"], lambda: vec.tensor_copy(T.oh[:, 256:512], T.oh[:, 0:256]))
-    vs("c_oh2", 256, ["oh0", "oh1"], ["oh2"], lambda: vec.tensor_copy(T.oh[:, 512:1024], T.oh[:, 0:512]))
-    vs("c_oh3", 512, ["oh0", "oh1", "oh2"], ["ohb"], lambda: vec.tensor_copy(T.oh[:, 1024:2048], T.oh[:, 0:1024]))
-    op("c_oh4", "a", "op", 1024, ["oh0", "oh1", "oh2"], ["ohi"],
-       lambda: act.activation(T.oh[:, 2048:3072], T.oh[:, 0:1024], AF.Copy))
-    vs("c_pk3", 32, ["pk2", "oh0"], ["pk3"], lambda: vec.tensor_tensor(T.pk3[:], T.pk2[:], T.oh[:, 0:16], ALU.mult))
-    vs("c_wcol", 16, ["pk3"], ["wcol"], lambda: vec.tensor_reduce(T.wcol[:], T.pk3[:, 0:12], AxisListType.X, ALU.add))
-    vs("c_zo", 144, ["x143", "gcol"], ["zo"], lambda: vec.tensor_scalar(T.zo[:], T.x143[:], T.gcol[:], None, ALU.is_equal))
-    vs("c_zc", 144, ["x143", "gcol", "wcol"], ["zc"],
-       lambda: vec.tensor_scalar(T.zc[:], T.x143[:], T.gcol[:], T.wcol[:], ALU.is_equal, ALU.mult))
-    vs("c_zp", 144, ["x143", "gcol"], ["zp"], lambda: vec.tensor_scalar(T.zp[:], T.x143[:], T.gcol[:], BIG, ALU.is_equal, ALU.mult))
-    vs("c_zn", 144, ["x143", "gcol"], ["zn"], lambda: vec.tensor_scalar(T.zn[:], T.x143[:], T.gcol[:], -BIG, ALU.is_equal, ALU.mult))
-    vs("c_idp", 128, ["x143", "pcol"], ["idp"], lambda: vec.tensor_scalar(T.idp[:], T.x143[:, 15:143], T.pcol[:], None, ALU.is_equal))
-    vs("c_idn", 128, ["x143", "pcol"], ["idn"],
-       lambda: vec.tensor_scalar(T.idn[:], T.x143[:, 15:143], T.pcol[:], -1.0, ALU.is_equal, ALU.mult))
-    vs("c_uc2", 48, ["uc1b", "uc1i", "rcol"], ["uc2"],
-       lambda: vec.tensor_scalar(T.uc2[:], T.uc1[:], 0.0, T.rcol[:], ALU.mult, ALU.add))
-    vs("c_b0", 1, ["thi"], ["b0"], lambda: vec.tensor_scalar(T.b0[:], T.thi[:], -1.0, -0.5, ALU.mult, ALU.add))
-    op("c_sum", "p", "mm", 64, ["am", "one"], ["pki"], lambda: pe.matmul(T.pki[:, 256:257], T.am[:], T.one[:], True, True))
-    vs("c_b1", 1, ["pki", "b0"], ["b1"], lambda: vec.tensor_scalar(T.b1[:], T.pki[:, 256:257], -256.0, T.b0[:], ALU.mult, ALU.add))
+    def ac(name, reads, writes, fn, banks=()):
+        op(name, "a", "op", reads, writes, fn, None, banks)
+
+    def mm(name, reads, bank, fn):
+        op(name, "p", "mm", reads, [], fn, None, (bank,))
+
+    def affine(name, e, out, in_, scale, bias, reads, writes, banks=()):
+        if e == "v":
+            vs(name, reads, writes, lambda: vec.tensor_scalar(out, in_, scale, bias, ALU.mult, ALU.add), banks)
+        else:
+            ac(name, reads, writes, lambda: act.activation(out, in_, AF.Copy, bias=bias, scale=scale), banks)
+
+    def gather(name, e, out, win, off, reads, writes):
+        if e == "v":
+            op(name, "v", "gat", reads, writes, lambda: vec.tensor_copy(out, win.indirect(off)))
+        else:
+            op(name, "a", "gat", reads, writes, lambda: act.activation(out, win.indirect(off), AF.Copy))
+
+    def psum(place, a, n):
+        return T["bank%d" % place[0]][:, place[1] + a:place[1] + a + n]
 
     others = [c for c in T.cores if c != core]
     near = [c for c in others if c in topo.cores_of(core)]
@@ -116,10 +138,10 @@ def build_ops(g, T, topo, core, rank, cfg):
         k = len(fe) // len(far)
         eng[c] = fe[i * k:(i + 1) * k]
     for c in near:
-        eng[c] = [e for e in topo.engines(core, c) if e not in fe]
+        eng[c] = [e for e in topo.engines(core, c) if e not in fe][::cfg["near"]]
     total = sum(len(x) for x in eng.values())
 
-    def send(name, ap, rsem, lsem, reads, arrives, kind):
+    def send(name, ap, rsem, lsem, reads, arrives):
         def fn():
             trs = []
             for c in far + near:
@@ -127,172 +149,318 @@ def build_ops(g, T, topo, core, rank, cfg):
                 trs.append(RemoteDMATransfer(dst_ids=[DstId(rid=rid, pnc=pid)], dma_engine_mask=sum(1 << e for e in eng[c]),
                                              remote_sem=T.sem[rsem], src=ap, dst=ap))
             return g.remote_dma_fused(trs, local_sem=T.sem[lsem])
-        op(name, "g", kind, total, reads, [arrives], fn, (rsem, lsem))
+        op(name, "g", "send", reads, arrives, fn, (rsem, lsem, total))
 
-    CH = [dict(blocks=[0], c0=0, k=32, bank="pkb", pw0=32 * rank, pwn=128, wn=M),
-          dict(blocks=[1], c0=32, k=32, bank="pki", pw0=128, pwn=192, wn=M + V - B),
-          dict(blocks=[2], c0=64, k=32, bank="pe2", pw0=160, pwn=192, wn=M + V - B)]
-    EB = [0, 1, 0]
-
-    def own(r, b):
+    def own(r, c0, k):
         if r == RO:
-            return T.fin[:, B * b:B * (b + 1)]
-        a = own0 if b == 0 else INN + B * (b - 1)
-        return W[r][:, a:a + B]
+            return T.fin[:, 16 * c0:16 * (c0 + k)]
+        a = (own0 if c0 < 32 else INN - B) + 16 * c0
+        return W[r][:, a:a + 16 * k]
 
-    def pm(r, ci):
-        ch = CH[ci]
+    def pm(r, c0, k):
         if r == RO:
-            return T.pfin[:, ch["c0"]:ch["c0"] + ch["k"]]
-        return PW[r][:, ch["pw0"]:ch["pw0"] + ch["k"]]
+            return T.pfin[:, c0:c0 + k]
+        a = (32 * rank if c0 < 32 else 96) + c0
+        return PW[r][:, a:a + k]
 
-    def wrap(name, ci, col, z, src, skey, first):
-        ch = CH[ci]
-        k, a = ch["k"], 16 * ch["c0"]
-        out = T[ch["bank"]][:, col:col + k]
+    def wk(r, ci):
+        return [("w", r, ci, 0), ("w", r, ci, 1)]
 
-        def fn():
-            last = None
-            for r in range(16):
-                last = pe.matmul(out, T[z][:, 15 - r:143 - r], src[:, a + r:a + 16 * k:16], first and r == 0, r == 15)
-            return last
-        op(name, "p", "mm", 16 * 64, [z] + [(skey, b) for b in ch["blocks"]], [ch["bank"]], fn)
-        return out
+    load("par", "s", T.pari[:], T.par[:], ["pari"])
+    load("qb", "a", W[0][:, own0:own0 + B], T.q[:, 0:B], [x for i in BORDER for x in wk(0, i)])
+    vs("pm0", ["pari"], [("pw", 0, i) for i in BORDER], lambda: vec.tensor_scalar(pm(0, 0, 32), T.pari[:, 0:32], -float(CEN), None, ALU.add))
+    send("sp_0", pm(0, 0, 32), "ap0", "lp0", [("pw", 0, i) for i in BORDER], [("pr", 0)])
+    send("sq_0_0", own(0, 0, 32), "aq0_0", "lq0_0", [x for i in BORDER for x in wk(0, i)], [("wr", 0, 0), ("wr", 0, 1)])
+    vs("pm1", ["pari"], [("pw", 0, i) for i in INNER], lambda: vec.tensor_scalar(pm(0, 32, 64), T.pari[:, 32:96], -float(CEN), None, ALU.add))
+    load("qi", "s", W[0][:, INN:DUP], T.q[:, B:V], [x for i in INNER for x in wk(0, i)])
+    load("am", "a", T.am[:], T.amat[:], ["am"])
+    load("clr", "s", T.clrs[:, 0:C // 2], T.clr[:, 0:C // 2], ["clrs"])
+    load("clr2", "s", T.clrs[:, C // 2:C], T.clr[:, C // 2:C], ["clrs2"])
+    load("th", "a", T.thi[:], T.th[:], ["thi"])
+    load("qdb", "s", W[0][:, 0:B], T.q[:, 0:B], [("wd", 0, 0)])
+    load("qdi", "s", W[0][:, DUP:WW], T.q[:, B:V], [("wd", 0, 1)])
 
-    def gather(name, out, win, off, reads, writes):
-        if name in cfg:
-            op(name, "v", "gat", B, reads, writes, lambda: vec.tensor_copy(out, win.indirect(off)))
-        else:
-            op(name, "a", "gat", B, reads, writes, lambda: act.activation(out, win.indirect(off), AF.Copy))
+    gp("i_p", "pci", lambda: g.iota(T.pci[:], [[0, 1]], 0, 1))
+    gp("i_16", "x16", lambda: g.iota(T.x16[:], [[0, 16], [1, 16]], 0, 0, allow_small_or_imprecise_dtypes=True))
+    gp("i_143", "x143", lambda: g.iota(T.x143[:], [[1, 144]], -15, 0, allow_small_or_imprecise_dtypes=True))
+    gp("i_u1", "uc1b", lambda: g.iota(T.uc1[:, 0:32], [[16, 32]], 0, 0, allow_small_or_imprecise_dtypes=True))
+    gp("i_u2", "uc1i", lambda: g.iota(T.uc1[:, 32:96], [[16, 64]], NAMES, 0, allow_small_or_imprecise_dtypes=True))
+    vs("c_two", [], ["two"], lambda: vec.memset(T.two[:], 2.0))
+    vs("c_zero", [], ["zero"], lambda: vec.memset(T.zero[:], 0.0))
+    vs("c_one", [], ["one"], lambda: vec.memset(T.one[:], 1.0))
+    vs("c_pk2", ["two", "zero"], ["pk2"], lambda: vec.tensor_tensor_scan(T.pk2[:], T.two[:], T.zero[:], 0.25, ALU.mult, ALU.add))
+    vs("c_rci", ["pci"], ["rci"], lambda: vec.tensor_scalar(T.rci[:], T.pci[:], 15, None, ALU.bitwise_and))
+    vs("c_rcol", ["rci"], ["rcol"], lambda: vec.tensor_copy(T.rcol[:], T.rci[:]))
+    vs("c_pcol", ["pci"], ["pcol"], lambda: vec.tensor_copy(T.pcol[:], T.pci[:]))
+    vs("c_gcol", ["pcol", "rcol"], ["gcol"], lambda: vec.tensor_tensor(T.gcol[:], T.pcol[:], T.rcol[:], ALU.subtract))
+    vs("c_oh0", ["x16", "rcol"], ["oh0"], lambda: vec.tensor_scalar(T.oh[:, 0:256], T.x16[:], T.rcol[:], None, ALU.is_equal))
+    vs("c_oh1", ["oh0"], ["oh1"], lambda: vec.tensor_copy(T.oh[:, 256:512], T.oh[:, 0:256]))
+    vs("c_oh2", ["oh0", "oh1"], ["oh2"], lambda: vec.tensor_copy(T.oh[:, 512:1024], T.oh[:, 0:512]))
+    vs("c_oh3", ["oh0", "oh1", "oh2"], ["ohb"], lambda: vec.tensor_copy(T.oh[:, 1024:2048], T.oh[:, 0:1024]))
+    if maski:
+        ac("c_oh4", ["oh0", "oh1", "oh2"], ["ohi"], lambda: act.activation(T.oh[:, 2048:3072], T.oh[:, 0:1024], AF.Copy))
+    vs("c_pk3", ["pk2", "oh0"], ["pk3"], lambda: vec.tensor_tensor(T.pk3[:], T.pk2[:], T.oh[:, 0:16], ALU.mult))
+    vs("c_wcol", ["pk3"], ["wcol"], lambda: vec.tensor_reduce(T.wcol[:], T.pk3[:, 0:12], AxisListType.X, ALU.add))
+    vs("c_zo", ["x143", "gcol"], ["zo"], lambda: vec.tensor_scalar(T.zo[:], T.x143[:], T.gcol[:], None, ALU.is_equal))
+    vs("c_zc", ["x143", "gcol", "wcol"], ["zc"],
+       lambda: vec.tensor_scalar(T.zc[:], T.x143[:], T.gcol[:], T.wcol[:], ALU.is_equal, ALU.mult))
+    vs("c_zp", ["zo"], ["zp"], lambda: vec.tensor_scalar(T.zp[:], T.zo[:], BIG, None, ALU.mult))
+    vs("c_zn", ["zo"], ["zn"], lambda: vec.tensor_scalar(T.zn[:], T.zo[:], -BIG, None, ALU.mult))
+    vs("c_idp", ["x143", "pcol"], ["idp"], lambda: vec.tensor_scalar(T.idp[:], T.x143[:, 15:143], T.pcol[:], None, ALU.is_equal))
+    vs("c_idk", ["idp"], ["idk"], lambda: vec.tensor_scalar(T.idk[:], T.idp[:], PK, None, ALU.mult))
+    if any(ch["T2"].strip("e") for ch in CH):
+        vs("c_idn", ["idp"], ["idn"], lambda: vec.tensor_scalar(T.idn[:], T.idp[:], -1.0, None, ALU.mult))
+    if any("e" in ch["T2"] for ch in CH):
+        vs("c_am2", ["am"], ["am2"], lambda: vec.tensor_scalar(T.am2[:], T.am[:], 2.0, None, ALU.mult))
+    vs("c_uc2", ["uc1b", "uc1i", "rcol"], ["uc2"], lambda: vec.tensor_scalar(T.uc2[:], T.uc1[:], -MID, T.rcol[:], ALU.add, ALU.add))
+    vs("c_idh", ["idp"], ["idh"], lambda: vec.tensor_copy(T.idh[:], T.idp[:]))
+    if rows:
+        vs("c_nr0", [], ["nr0"], lambda: vec.memset(T.nr[:, 0:NAMES // 2], 0.0))
+        ac("c_nr1", ["nr0"], ["nr"], lambda: act.activation(T.nr[:, NAMES // 2:NAMES], T.nr[:, 0:NAMES // 2], AF.Copy))
+        vs("c_idw", ["idp"], ["idw"], lambda: vec.tensor_scalar(T.idw[:], T.idp[:], float(LW), None, ALU.mult))
+        vs("c_idm", ["idp"], ["idm"], lambda: vec.tensor_scalar(T.idm[:], T.idp[:], -16.0 * LW, None, ALU.mult))
+    sb = CH[INNER[0]]["ls"][0]
+    vs("c_b0", ["thi"], ["b0"], lambda: vec.tensor_scalar(T.b0[:], T.thi[:], -1.0, -0.5, ALU.mult, ALU.add))
+    mm("c_sum", ["am", "one"], sb, lambda: pe.matmul(T["bank%d" % sb][:, 500:501], T.am[:], T.one[:], True, True))
+    vs("c_b1", ["b0"], ["b1"], lambda: vec.tensor_scalar(T.b1[:], T["bank%d" % sb][:, 500:501], -256.0, T.b0[:], ALU.mult, ALU.add), (sb,))
+    if any("v" in ch["T3"] for ch in CH):
+        vs("c_n1", ["b1", "pk2"], ["n1"], lambda: vec.tensor_scalar(T.nth[:, 1:RO], T.pk2[:, 2:RO + 1], T.b1[:], -1.0, ALU.mult, ALU.mult))
+        vs("c_n0", ["b0"], ["n0"], lambda: vec.tensor_scalar(T.nth[:, 0:1], T.b0[:], -1.0, None, ALU.mult))
+    for i, ch in enumerate(CH):
+        if len(set(ch["T3"])) > 1:
+            for j in range(2):
+                ap = T.half[:, ch["c0"] + j * ch["k"] // 2:ch["c0"] + (j + 1) * ch["k"] // 2]
+                vs("c_half%d%d" % (i, j), [], [("half", i)], lambda ap=ap, x=2048.0 * (ch["T3"][j] == "a"): vec.memset(ap, x))
 
-    def ab(r, b):
-        return T[("ah%d" if "T7_%d_%d" % (r, b) in cfg else "ab%d") % b][:]
+    def span(cis):
+        c0, k = CH[cis[0]]["c0"], sum(CH[i]["k"] for i in cis)
+        return c0, k, slice(c0, c0 + k)
 
-    def halves(r, b):
-        out, bias, src = ab(r, b), (255.75 if r == 0 else -0.25 * 2 ** r), own(r, b)
-        if "T7_%d_%d" % (r, b) in cfg:
-            vs("T7_%d_%d" % (r, b), B // 2, [("w", r, b)], [("ab", b)],
-               lambda: vec.tensor_scalar(out, src, bias, None, ALU.add))
-        else:
-            op("T7_%d_%d" % (r, b), "a", "op", B, [("w", r, b)], [("ab", b)],
-               lambda: act.activation(out, src, AF.Copy, bias=bias))
+    def lists(r, cis, step):
+        c0, k, cs = span(cis)
+        t, p, pk = "_%d_%d" % (r, cis[0]), pm(r, c0, k), [("pw", r, i) for i in cis]
+        if step == "kp":
+            affine("kp" + t, cfg["kp"], T.keep[:, cs], p, PK + 1, PK * (CEN - MID + (OFF if c0 < 32 else 0)), pk, [("keep", i) for i in cis])
+        elif step == "up" and any(CH[i]["names"] == "mask" for i in cis):
+            vs("up" + t, pk, [("up", i) for i in cis], lambda: vec.tensor_scalar(T.up[:, cs], p, float(CEN), None, ALU.add))
+        elif step == "u4" and any(CH[i]["names"] == "mask" for i in cis):
+            vs("u4" + t, pk, [("u4", i) for i in cis],
+               lambda: vec.tensor_scalar(T.u4[:, cs], p, 1.0 / 16, CEN / 16 - 15.0 / 32, ALU.mult, ALU.add))
+        elif step == "un" and any(CH[i]["names"] == "rows" for i in cis):
+            ls = CH[cis[-1]]["ls"]
+            o = psum(ls, 192, k)
+            vs("h4" + t, pk, [("h4", cis[0])],
+               lambda: vec.tensor_scalar(T.h4[:, cs], p, 1.0 / 16, CEN / 16 + 1100 - 15.0 / 32, ALU.mult, ALU.add))
 
-    def chunk_round(r, ci):
-        ch = CH[ci]
-        k, c0, bank, blocks = ch["k"], ch["c0"], ch["bank"], ch["blocks"]
+            def place():
+                pe.matmul(o, T.idw[:], p, True, False)
+                pe.matmul(o, T.idm[:], T.h4[:, cs], False, False)
+                return pe.matmul(o, T.idh[:], T.h4[:, cs], False, True)
+            mm("nm" + t, pk + [("h4", cis[0]), "idw", "idm", "idh"], ls[0], place)
+            vs("un" + t, [], [("un", i) for i in cis],
+               lambda: vec.tensor_scalar(T.un[:, cs], o, 1.0 * CEN * LW + 1100.0 * (16 * LW - 1), None, ALU.add), (ls[0],))
+
+    def parents(r, cis):
+        c0, k, cs = span(cis)
+        t = "_%d_%d" % (r, cis[0])
+        last = r + 1 == RO
+        vs("tt" + t, [("sl", i) for i in cis], [("tt", cis[0])],
+           lambda: vec.tensor_scalar(T.tt[:, cs], T.sl[:, cs], SNAP, -SNAP - (CEN if last else 0), ALU.add, ALU.add) if not last else
+           vec.tensor_scalar(T.tt[:, cs], T.us[:, cs], PK, -PK * MID - CEN, ALU.mult, ALU.add))
+        if last:
+            ops[-1]["reads"] = [("us", i) for i in cis]
+        vs("pn" + t, [("tt", cis[0])] + [("sl", i) for i in cis], [("pw", r + 1, i) for i in cis],
+           lambda: vec.tensor_tensor(pm(r + 1, c0, k), T.sl[:, cs], T.tt[:, cs], ALU.subtract))
+        if last:
+            dma("styp%d" % cis[0], cfg["stq"], T.yp[:, cs], pm(RO, c0, k), [("pw", RO, i) for i in cis], [], "st%d" % (8 + cis[0]))
+
+    def block_round(r, ci, stage, together):
+        ch = dict(CH[ci], **CH[ci].get("at", {}).get(r, {}))
+        k, c0, ls = ch["k"], ch["c0"], ch["ls"]
+        inner = c0 >= 32
         t = "_%d_%d" % (r, ci)
-        cs = slice(c0, c0 + k)
-        p = pm(r, ci)
-        pk = ("pw", r, ci)
-        wkeys = [("w", r, 0), ("wr", r)] + ([("w", r, 1), ("w", r, 2)] if ci else [])
-        pkeys = [("pw", r, 0), ("pr", r)] + ([("pw", r, 1), ("pw", r, 2)] if ci else [])
-        ohk = ["oh0", "oh1", "oh2", "ohb"] + (["ohi"] if ci else [])
-        inv = 1.0 / 2 ** r
-        vs("up" + t, k, [pk], [("up", ci)], lambda: vec.tensor_scalar(T.up[:, cs], p, 1024.0, None, ALU.add))
-        vs("u4" + t, k, [pk], [("u4", ci)],
-           lambda: vec.tensor_scalar(T.u4[:, cs], p, 1.0 / 16, 64 - 15.0 / 32, ALU.mult, ALU.add))
-        for b in blocks:
-            if b != 1:
-                halves(r, b)
-        for b in blocks:
-            bs, os_ = slice(B * b, B * (b + 1)), slice(32 * b, 32 * (b + 1))
-            gather("T8_%d_%d" % (r, b), T.msk[:, bs], T.oh[:, 0:ch["wn"]], T.up[:, os_], ohk + [("up", ci)], [("msk", b)])
-            op("T1_%d_%d" % (r, b), "v", "gat", B, pkeys + [("u4", ci), ("msk", b)], [("cand", b)],
-               lambda bs=bs, os_=os_: vec.tensor_tensor(T.cand[:, bs], PW[r][:, 0:ch["pwn"]].indirect(T.u4[:, os_]),
-                                                        T.msk[:, bs], ALU.mult))
-            op("sa_%d_%d" % (r, b), "p", "mm", B, ["am", ("w", r, b)], [("ps", b)],
-               lambda b=b: pe.matmul(T["ps%d" % b][:], T.am[:], own(r, b), True, False))
-        hm = wrap("wh" + t, ci, 0, "zo", T.cand, "cand", True)
-        vs("uh" + t, k, [bank], [("uh", ci)], lambda: vec.tensor_scalar(T.uh[:, cs], hm, 1024.0, None, ALU.add))
-        vs("dh" + t, k, [bank, pk], [("dh", ci)], lambda: vec.tensor_tensor(T.dh[:, cs], hm, p, ALU.subtract))
-        bias = T.b0 if r == 0 else T.b1
-        for b in blocks:
-            bs, os_ = slice(B * b, B * (b + 1)), slice(32 * b, 32 * (b + 1))
-            gather("T2_%d_%d" % (r, b), T.dd[:, bs], W[r][:, OFF:OFF + ch["wn"]], T.uh[:, os_], wkeys + [("uh", ci)], [("dd", b)])
-            op("sd_%d_%d" % (r, b), "p", "mm", B, ["am", ("dd", b)], [("ps", b)],
-               lambda b=b, bs=bs: pe.matmul(T["ps%d" % b][:], T.am[:], T.dd[:, bs], False, True))
-            eb = T["pe%d" % EB[b]][:]
-            op("ea_%d_%d" % (r, b), "p", "mm", B, ["idp", ("w", r, b)], [("pe", EB[b])],
-               lambda b=b, eb=eb: pe.matmul(eb, T.idp[:], own(r, b), True, False))
-            op("ed_%d_%d" % (r, b), "p", "mm", B, ["idn", ("dd", b)], [("pe", EB[b])],
-               lambda bs=bs, eb=eb: pe.matmul(eb, T.idn[:], T.dd[:, bs], False, True))
-            op("T3_%d_%d" % (r, b), "a", "op", B, [("ps", b), "b0", "b1"], [("sg", b)],
-               lambda b=b, bs=bs: act.activation(T.sg[:, bs], T["ps%d" % b][:], AF.Sign, bias=bias[:], scale=inv))
-            op("T4_%d_%d" % (r, b), "a", "op", B, [("pe", EB[b])], [("ae", b)],
-               lambda eb=eb, bs=bs: act.activation(T.ae[:, bs], eb, AF.Abs, scale=inv))
-        cd = wrap("wc" + t, ci, 64, "zc", T.sg, "sg", True)
-        vs("uc" + t, k, [bank], [("uc", ci)], lambda: vec.tensor_scalar(T.uc[:, cs], cd, 2047.5, None, ALU.add))
-        u = T[bank][:, 128:128 + k]
+        cs, wn = slice(c0, c0 + k), (NAMES if inner else M)
+        seen = list(range(len(CH))) if inner else BORDER
+        wkeys = [x for i in seen for x in wk(r, i)] + [("wr", r, 0), ("wr", r, 1)]
+        pkeys = [("pw", r, i) for i in seen] + [("pr", r)]
+        inv, bias = 1.0 / 2 ** r, (255.75 if r == 0 else -0.25 * 2 ** r)
+        win = W[r][:, OFF:OFF + wn]
+        wide = W[r][:, OFF:WW] if inner else W[r][:, 0:INN]
 
-        def consts():
-            pe.matmul(u, T.idp[:], T.uc1[:, cs], True, False)
-            return pe.matmul(u, T.idp[:], T.uc2[:, cs], False, False)
-        op("uk" + t, "p", "mm", 128, ["idp", "uc1b", "uc1i", "uc2"], [bank], consts)
-        for b in blocks:
-            bs, os_ = slice(B * b, B * (b + 1)), slice(32 * b, 32 * (b + 1))
-            op("T5_%d_%d" % (r, b), "v", "gat", B, ["clrs", ("uc", ci), ("ae", b)], [("viol", b)],
-               lambda bs=bs, os_=os_: vec.tensor_tensor(T.viol[:, bs], T.clrs[:].indirect(T.uc[:, os_]), T.ae[:, bs], ALU.is_lt))
-        wrap("wu" + t, ci, 128, "zn" if ci else "zp", T.viol, "viol", False)
-        vs("sl" + t, k, [bank, pk], [("sl", ci)], lambda: vec.tensor_tensor(T.sl[:, cs], u, p, ALU.max if ci else ALU.min))
-        vs("ok" + t, k, [bank], [("ok", ci)],
-           lambda: vec.tensor_scalar(T.okf[:, cs], u, 0.0 if ci else -1024.5, None, ALU.is_gt if ci else ALU.is_lt))
-        vs("us" + t, k, [("sl", ci)], [("us", ci)],
-           lambda: vec.tensor_scalar(T.us[:, cs], T.sl[:, cs], 1024.0 if ci else 1024.0 + OFF, None, ALU.add))
-        vs("tt" + t, 2 * k, [("ok", ci), ("dh", ci)], [("tt", ci)],
-           lambda: vec.tensor_tensor(T.tt[:, cs], T.okf[:, cs], T.dh[:, cs], ALU.mult))
-        vs("pn" + t, 2 * k, [("tt", ci), pk], [("pw", r + 1, ci)], lambda: vec.tensor_tensor(pm(r + 1, ci), T.tt[:, cs], p, ALU.add))
-        if ci == 0 and r + 1 < RO:
-            send("sp%d" % (r + 1), pm(r + 1, 0), "ap%d" % (r + 1), "lp%d" % (r + 1), [("pw", r + 1, 0)], ("pr", r + 1), "sendp")
-        win = W[r][:, OFF:WW] if ci else W[r][:, 0:INN]
-        for b in blocks:
-            os_ = slice(32 * b, 32 * (b + 1))
-            if b == 1:
-                bs, q, bi = slice(B * b, B * (b + 1)), T["pe%d" % b][:], (255.75 if r == 0 else -0.25 * 2 ** r)
-                op("ma_%d_%d" % (r, b), "p", "mm", B, ["idp", ("w", r, b)], [("pe", b)],
-                   lambda b=b, q=q: pe.matmul(q, T.idp[:], own(r, b), True, False))
-                gather("G6_%d_%d" % (r, b), T.dd[:, bs], win, T.us[:, os_], wkeys + [("wd", r, ci), ("us", ci)], [("dd", b)])
-                op("mb_%d_%d" % (r, b), "p", "mm", B, ["idp", ("dd", b)], [("pe", b)],
-                   lambda bs=bs, q=q: pe.matmul(q, T.idp[:], T.dd[:, bs], False, True))
-                if "P6_%d_%d" % (r, b) in cfg:
-                    vs("P6_%d_%d" % (r, b), B, [("pe", b)], [("w", r + 1, b)],
-                       lambda b=b, q=q, bi=bi: vec.tensor_scalar(own(r + 1, b), q, bi, None, ALU.add))
-                else:
-                    op("P6_%d_%d" % (r, b), "a", "op", B, [("pe", b)], [("w", r + 1, b)],
-                       lambda b=b, q=q, bi=bi: act.activation(own(r + 1, b), q, AF.Copy, bias=bi))
-                continue
-            op("T6_%d_%d" % (r, b), "v", "gat", B, wkeys + [("wd", r, min(ci, 1)), ("us", ci), ("ab", b)], [("w", r + 1, b)],
-               lambda b=b, os_=os_: vec.tensor_tensor(own(r + 1, b), win.indirect(T.us[:, os_]), ab(r, b), ALU.add))
-        if r + 1 < RO:
-            if ci == 0:
-                send("sq%d" % (r + 1), own(r + 1, 0), "aq%d" % (r + 1), "lq%d" % (r + 1), [("w", r + 1, 0)], ("wr", r + 1), "sendq")
-                dma("db%d" % r, "s", W[r + 1][:, 0:B], own(r + 1, 0), [("w", r + 1, 0), ("wr", r + 1)], [("wd", r + 1, 0)],
-                    "db%d" % r, 300)
-            elif ci == 2:
-                dma("di%d" % r, "s", W[r + 1][:, DUP:WW], W[r + 1][:, INN:DUP], [("w", r + 1, 1), ("w", r + 1, 2)],
-                    [("wd", r + 1, 1)], "di%d" % r, 600)
-        else:
-            vs("yp" + t, k, [("pw", RO, ci)], [("yps", ci)], lambda: vec.tensor_scalar(T.yps[:, cs], pm(RO, ci), 1024.0, None, ALU.add))
-            dma("styp%d" % ci, "s", T.yp[:, cs], T.yps[:, cs], [("yps", ci)], [], "st%d" % (3 + ci), 0)
-            for b in blocks:
-                bs = slice(B * b, B * (b + 1))
-                if "fin%d" % b in cfg:
-                    vs("fin%d" % b, B // 2, [("w", RO, b)], [("yq", b)],
-                       lambda bs=bs: vec.tensor_scalar(T.yqs[:, bs], T.fin[:, bs], 1.0 / 2 ** RO, -128.0, ALU.mult, ALU.add))
-                else:
-                    op("fin%d" % b, "a", "op", B, [("w", RO, b)], [("yq", b)],
-                       lambda bs=bs: act.activation(T.yqs[:, bs], T.fin[:, bs], AF.Copy, bias=-128.0, scale=1.0 / 2 ** RO))
-                dma("styq%d" % b, "s", T.yq[:, bs], T.yqs[:, bs], [("yq", b)], [], "st%d" % b, 300)
+        def pieces(s):
+            h = k // len(s)
+            return [dict(x="b" if j else "", e=s[j], j=j, n=16 * h, cs=slice(c0 + j * h, c0 + (j + 1) * h),
+                         bs=slice(16 * (c0 + j * h), 16 * (c0 + (j + 1) * h)), a=own(r, c0 + j * h, h), new=own(r + 1, c0 + j * h, h),
+                         js=[j] if len(s) > 1 else [0, 1]) for j in range(len(s))]
 
-    vs("pm0", 32, ["pari"], [("pw", 0, 0)], lambda: vec.tensor_scalar(pm(0, 0), T.pari[:, 0:32], -1024.0, None, ALU.add))
-    send("sp0", pm(0, 0), "ap0", "lp0", [("pw", 0, 0)], ("pr", 0), "sendp")
-    send("sq0", own(0, 0), "aq0", "lq0", [("w", 0, 0)], ("wr", 0), "sendq")
-    vs("pm1", 64, ["pari"], [("pw", 0, 1), ("pw", 0, 2)],
-       lambda: vec.tensor_scalar(PW[0][:, 128:192], T.pari[:, 32:96], -1024.0, None, ALU.add))
+        def keys(b, h=None):
+            return [(b, ci, j) for j in (h["js"] if h else [0, 1])]
+
+        def mine(q, h):
+            return [("w", q, ci, j) for j in h["js"]]
+
+        def over_groups(out, z, src, first, last, n=k):
+            for j in range(16):
+                ins = pe.matmul(out, T[z][:, 15 - j:143 - j], src[:, 16 * c0 + j:16 * (c0 + n):16], first and j == 0, last and j == 15)
+            return ins
+
+        def names(h):
+            op(h["x"] + "T1" + t, "v", "gat", pkeys + [("u4", ci)] + keys("msk", h), keys("cand", h),
+               lambda: vec.tensor_tensor(T.cand[:, h["bs"]], PW[r][:, 0:wn // 16].indirect(T.u4[:, h["cs"]]), T.msk[:, h["bs"]], ALU.mult))
+
+        banks = pieces(ch["T3"])
+        for h in banks:
+            h["ps"], h["pd"], h["diff"] = ch["ps"][h["j"]], ch["pe"][h["j"]], ch["T2"][min(h["j"], len(ch["T2"]) - 1)] == "e"
+
+        def sa(h):
+            mm(h["x"] + "sa" + t, ["am", "am2"] + mine(r, h), h["ps"][0],
+               lambda: pe.matmul(psum(h["ps"], 0, h["n"]), (T.am2 if h["diff"] else T.am)[:], h["a"], True, False))
+
+        def grand(h):
+            d = T.dd[:, h["bs"]]
+            if h["e"] == "e":
+                if ch.get("dup"):
+                    a2, src = W[r][:, DUP - B + h["bs"].start:DUP - B + h["bs"].stop], [("wd", r, 1)]
+                else:
+                    a2, src = T.aa[:, h["bs"]], keys("aa", h)
+                    vs(h["x"] + "cp" + t, mine(r, h), src, lambda: vec.tensor_copy(a2, h["a"]))
+                op(h["x"] + "T2" + t, "v", "gat", wkeys + [("uh", ci)] + src, keys("dd", h),
+                   lambda: vec.tensor_tensor(d, win.indirect(T.uh[:, h["cs"]]), a2, ALU.subtract))
+            else:
+                gather(h["x"] + "T2" + t, h["e"], d, win, T.uh[:, h["cs"]], wkeys + [("uh", ci)], keys("dd", h))
+
+        def bits(h):
+            x, d, ps, pd = h["x"], T.dd[:, h["bs"]], psum(h["ps"], 0, h["n"]), psum(h["pd"], 0, h["n"])
+            mm(x + "sd" + t, ["am"] + keys("dd", h), h["ps"][0], lambda: pe.matmul(ps, T.am[:], d, False, True))
+            if not h["diff"]:
+                mm(x + "ea" + t, ["idp"] + mine(r, h), h["pd"][0], lambda: pe.matmul(pd, T.idp[:], h["a"], True, False))
+                mm(x + "ed" + t, ["idn"] + keys("dd", h), h["pd"][0], lambda: pe.matmul(pd, T.idn[:], d, False, True))
+            if h["e"] == "a":
+                th = T.b0 if r == 0 else T.b1
+                ac(x + "T3" + t, ["b0", "b1"], keys("sg", h),
+                   lambda: act.activation(T.sg[:, h["bs"]], ps, AF.Sign, bias=th[:], scale=inv), (h["ps"][0],))
+            else:
+                vs(x + "T3" + t, ["n0", "n1"], keys("sg", h),
+                   lambda: vec.tensor_scalar(T.sg[:, h["bs"]], ps, T.nth[:, r:r + 1], 2.0, ALU.is_gt, ALU.mult), (h["ps"][0],))
+            if h["diff"]:
+                ac(x + "T4" + t, keys("dd", h), keys("ae", h), lambda: act.activation(T.ae[:, h["bs"]], d, AF.Abs, scale=inv))
+            else:
+                ac(x + "T4" + t, [], keys("ae", h), lambda: act.activation(T.ae[:, h["bs"]], pd, AF.Abs, scale=inv), (h["pd"][0],))
+
+        def room(h):
+            op(h["x"] + "T5" + t, "v", "gat", ["clrs", "clrs2", ("uc", ci)] + keys("ae", h), keys("viol", h),
+               lambda: vec.tensor_tensor(T.viol[:, h["bs"]], T.clrs[:].indirect(T.uc[:, h["cs"]]), T.ae[:, h["bs"]], ALU.is_lt))
+
+        def quarter(h):
+            return (T.ah if ch["T7"][h["j"]] == "v" else T.ab)[:, h["bs"]]
+
+        def update(h):
+            x, j, rd = h["x"], h["j"], wkeys + [("wd", r, int(inner)), ("us", ci)]
+            if h["e"] == "T":
+                op(x + "T6" + t, "v", "gat", rd + keys("ab", h), mine(r + 1, h),
+                   lambda: vec.tensor_tensor(h["new"], wide.indirect(T.us[:, h["cs"]]), quarter(h), ALU.add))
+                return
+            ps = ch["pu"][j]
+            q = psum(ps, 0, h["n"])
+            mm(x + "ma" + t, ["idp"] + mine(r, h), ps[0], lambda: pe.matmul(q, T.idp[:], h["a"], True, False))
+            gather(x + "G6" + t, ch["G6"][j], T.gg[:, h["bs"]], wide, T.us[:, h["cs"]], rd, keys("gg", h))
+            mm(x + "mb" + t, ["idp"] + keys("gg", h), ps[0], lambda: pe.matmul(q, T.idp[:], T.gg[:, h["bs"]], False, True))
+            affine(x + "P6" + t, ch["P6"][j], h["new"], q, 1.0, bias, [], mine(r + 1, h), (ps[0],))
+
+        if stage == "names":
+            for h in pieces(ch["upd"]):
+                if h["e"] == "T":
+                    affine(h["x"] + "T7" + t, ch["T7"][h["j"]], quarter(h), h["a"], 1.0, bias, mine(r, h), keys("ab", h))
+            if ch["names"] == "mask":
+                for h in pieces(ch["T8"]):
+                    gather(h["x"] + "T8" + t, h["e"], T.msk[:, h["bs"]], T.oh[:, 0:wn], T.up[:, h["cs"]],
+                           ["oh0", "oh1", "oh2", "ohb", ("up", ci)] + (["ohi"] if inner else []), keys("msk", h))
+                for h in pieces(ch["T1"]):
+                    names(h)
+            else:
+                for h in pieces(ch["T1"]):
+                    gather(h["x"] + "T1" + t, h["e"], T.cand[:, h["bs"]], T.nr[:], T.un[:, h["cs"]], ["nr", ("un", ci)], keys("cand", h))
+            for h in banks:
+                if h["ps"][0] != ls[0]:
+                    sa(h)
+            return
+        lc = ch["ps"][0] if cfg["lc"] else (ls[0], ls[1] + k)
+        cd, u = psum(lc, 0, k), psum(ls, 0, k)
+        if together[0] == ci:
+            _, kk, cc = span(together)
+            hm = psum(ls, 128, kk)
+            mm("wh" + t, ["zo"] + [("cand", i, j) for i in together for j in (0, 1)], ls[0],
+               lambda: over_groups(hm, "zo", T.cand, True, True, kk))
+            vs("uh" + t, [], [("uh", i) for i in together],
+               lambda: vec.tensor_scalar(T.uh[:, cc], hm, float(CEN), None, ALU.add), (ls[0],))
+            vs("hc" + t, [], [("hs", i) for i in together], lambda: vec.tensor_copy(T.hs[:, cc], hm), (ls[0],))
+        for h in banks:
+            if h["ps"][0] == ls[0]:
+                sa(h)
+        for h in pieces(ch["T2"]):
+            grand(h)
+        for h in banks:
+            bits(h)
+        mixed = len(set(ch["T3"])) > 1
+
+        def code():
+            if mixed:
+                pe.matmul(cd, T.idp[:], T.half[:, cs], True, False)
+            return over_groups(cd, "zc", T.sg, not mixed, True)
+        mm("wc" + t, ["zc", ("half", ci)] + keys("sg"), lc[0], code)
+        vs("uc" + t, [], [("uc", ci)],
+           lambda: vec.tensor_scalar(T.uc[:, cs], cd, -0.25 if mixed else 2047.5 if ch["T3"][0] == "a" else 0.0, None, ALU.add), (lc[0],))
+
+        def granted():
+            pe.matmul(u, T.idk[:], T.uc2[:, cs], True, False)
+            return pe.matmul(u, T.idh[:], T.hs[:, cs], False, False)
+        mm("uk" + t, ["idk", "uc2", "idh", ("hs", ci)], ls[0], granted)
+        for h in pieces(ch["T5"]):
+            room(h)
+        z = "zn" if inner else "zp"
+        mm("wu" + t, [z] + keys("viol"), ls[0], lambda: over_groups(u, z, T.viol, False, True))
+        vs("sl" + t, [("keep", ci)], [("sl", ci)],
+           lambda: vec.tensor_tensor(T.sl[:, cs], u, T.keep[:, cs], ALU.max if inner else ALU.min), (ls[0],))
+        vs("us" + t, [("sl", ci)], [("us", ci)], lambda: vec.tensor_scalar(T.us[:, cs], T.sl[:, cs], 1 / PK, MID, ALU.mult, ALU.add))
+        for h in pieces(ch["upd"]):
+            update(h)
+        if r + 1 == RO:
+            for h in pieces(ch["fin"]):
+                s = "%s%d" % (h["x"], ci)
+                affine("fin" + s, h["e"], T.yqs[:, h["bs"]], T.fin[:, h["bs"]], 1.0 / 2 ** RO, -128.0, mine(RO, h), keys("yq", h))
+                dma("styq" + s, "s", T.yq[:, h["bs"]], T.yqs[:, h["bs"]], keys("yq", h), [], "st%d" % (2 * ci + h["j"]))
+        elif not inner:
+            for h in pieces(ch["upd"]):
+                send(h["x"] + "sq_%d_%d" % (r + 1, ci), h["new"], "aq%d_%d" % (r + 1, h["j"]), "lq%d_%d" % (r + 1, h["j"]),
+                     mine(r + 1, h), [("wr", r + 1, j) for j in h["js"]])
+
+    def sets(step, cis):
+        return [cis] if step in cfg["merge"] or cis is BORDER else [[i] for i in cis]
+
     for r in range(RO):
-        for ci in range(3):
-            chunk_round(r, ci)
+        if rows:
+            dma("nr_%d" % r, "s", T.nr[0:128:16, :], PW[r][:], [("pw", r, i) for i in range(len(CH))] + [("pr", r)], ["nr0", "nr"], "nr%d" % r)
+        for cis in (BORDER, INNER):
+            for step in ("kp", "up", "u4", "un"):
+                for x in sets(step, cis):
+                    lists(r, x, step)
+            for stage in ("names", "rest"):
+                for x in sets("wh", cis):
+                    for ci in x:
+                        block_round(r, ci, stage, x)
+            for x in sets("pn", cis):
+                parents(r, x)
+            if r + 1 == RO:
+                continue
+            if cis is BORDER:
+                send("sp_%d" % (r + 1), pm(r + 1, 0, 32), "ap%d" % (r + 1), "lp%d" % (r + 1), [("pw", r + 1, i) for i in BORDER], [("pr", r + 1)])
+                dma("db_%d" % r, "s", W[r + 1][:, 0:B], own(r + 1, 0, 32),
+                    [x for i in BORDER for x in wk(r + 1, i)] + [("wr", r + 1, 0), ("wr", r + 1, 1)], [("wd", r + 1, 0)], "db%d" % r)
+            else:
+                dma("di_%d" % r, "s", W[r + 1][:, DUP:WW], W[r + 1][:, INN:DUP], [x for i in INNER for x in wk(r + 1, i)],
+                    [("wd", r + 1, 1)], "di%d" % r)
 
-    writer, readers = {}, {}
+    writer, readers, turn = {}, {}, {}
     for i, o in enumerate(ops):
         d = set()
         for x in o["reads"]:
@@ -302,6 +470,14 @@ def build_ops(g, T, topo, core, rank, cfg):
             if x in writer:
                 d.add(writer[x])
             d.update(readers.get(x, []))
+        for b in o["banks"]:
+            e, now, before = turn.get(b, (None, [], []))
+            if e != o["eng"]:
+                now, before = [], now
+            d.update(before)
+            if o["eng"] == "p":
+                d.update(now[-1:])
+            turn[b] = (o["eng"], now + [i], before)
         d.discard(i)
         o["deps"] = sorted(d)
         for x in o["reads"]:
@@ -312,13 +488,29 @@ def build_ops(g, T, topo, core, rank, cfg):
     return ops
 
 
+def step_of(name):
+    p = name.split("_")
+    if len(p) == 1 or p[0] in ("c", "i", "l") or name in ("sp_0", "sq_0_0"):
+        return name, (RO - 1 if name[:3] in ("fin", "sty") else 0)
+    return ".".join(p[:1] + p[2:]), int(p[1]) - (p[0] in ("sp", "sq", "bsq"))
+
+
+def issue_order(ops, order):
+    steps = [(x.split("+")[0], int((x + "+0").split("+")[1])) for x in order.split()]
+    listed = [s for s, lag in steps]
+    index = {}
+    for i, o in enumerate(ops):
+        s, r = step_of(o["name"])
+        index[(s + "@%d" % r if s + "@%d" % r in listed else s, r)] = i
+    return [index[(s, t - lag)] for t in range(2 * RO) for s, lag in steps if (s, t - lag) in index]
+
+
 def rank_program(g, core, T, topo):
     rank = T.rank_of(core)
     if rank is None:
         return
     ops = build_ops(g, T, topo, core, rank, CFG)
-    loads = [i for i, o in enumerate(ops) if o["name"].startswith("l_")]
-    order = loads + [i for i in ORDER if i not in loads]
+    order = issue_order(ops, ORDER) if ORDER else list(range(len(ops)))
     queue = {"v": g.vector, "a": g.scalar, "p": g.tensor, "s": g.sync, "g": g}
     esem = {"v": "sv", "a": "sa", "p": "sp", "g": "sgp"}
     count, token, seen, ends = {}, {}, {}, {}
@@ -339,9 +531,9 @@ def rank_program(g, core, T, topo):
         if o["kind"] == "dma":
             ins.then_inc(T.sem[o["sem"]], 16)
             token[i] = (o["sem"], 16)
-        elif o["kind"] in ("sendp", "sendq"):
-            token[i] = (o["sem"][0], o["n"])
-            ends[o["sem"][1]] = o["n"]
+        elif o["kind"] == "send":
+            token[i] = (o["sem"][0], o["sem"][2])
+            ends[o["sem"][1]] = o["sem"][2]
         else:
             count[e] = count.get(e, 0) + 1
             ins.then_inc(T.sem[esem[e]], 1)

from concourse.bass import DstId, RemoteDMATransfer
from concourse.mybir import AluOpType as ALU, AxisListType, ActivationFunctionType as AF

N, V, B, RO, C = 4, 1536, 512, 5, 4096
M = N * B
OFF = B
INN = OFF + M
DUP = INN + V - B
WW = DUP + V - B
NAMES = M + V - B
LW = NAMES // 16
CEN = NAMES // 2
PK = 4096.0
MID = PK / 2
BIG = 2.0 ** 24
SNAP = 1.5 * 2.0 ** 35

SCRATCH = {}
for _r in range(RO):
    SCRATCH["w%d" % _r] = ("sbuf", [128, WW], "bfloat16")
    SCRATCH["pw%d" % _r] = ("sbuf", [128, LW], "float32")
for _n, _w, _d in [
    ("fin", V, "bfloat16"), ("yqs", V, "bfloat16"), ("pfin", 96, "float32"), ("yps", 96, "float32"),
    ("clrs", C, "bfloat16"), ("am", 128, "bfloat16"), ("am2", 128, "bfloat16"), ("thi", 1, "int32"), ("pari", 96, "int32"),
    ("oh", NAMES, "bfloat16"), ("nr", NAMES, "float32"), ("msk", V, "bfloat16"), ("cand", V, "float16"), ("dd", V, "bfloat16"),
    ("gg", V, "bfloat16"), ("aa", V, "bfloat16"), ("sg", V, "bfloat16"), ("ae", V, "bfloat16"), ("viol", V, "bfloat16"),
    ("ab", V, "float32"), ("ah", V, "float16"),
    ("u4", 96, "uint16"), ("up", 96, "uint16"), ("uh", 96, "uint16"), ("uc", 96, "uint16"), ("us", 96, "uint16"),
    ("un", 96, "uint16"), ("h4", 96, "float16"),
    ("keep", 96, "float32"), ("hs", 96, "float16"), ("sl", 96, "float32"), ("tt", 96, "float32"),
    ("pci", 1, "int32"), ("rci", 1, "int32"), ("pcol", 1, "float32"), ("rcol", 1, "float32"), ("gcol", 1, "float32"),
    ("wcol", 1, "float32"), ("b0", 1, "float32"), ("b1", 1, "float32"), ("nth", 8, "float32"), ("half", 96, "bfloat16"),
    ("one", 1, "bfloat16"),
    ("x143", 144, "float32"), ("x16", 256, "bfloat16"), ("two", 16, "float32"), ("zero", 16, "float32"),
    ("pk2", 16, "float32"), ("pk3", 16, "float32"),
    ("zc", 144, "bfloat16"), ("zo", 144, "float16"), ("zp", 144, "bfloat16"), ("zn", 144, "bfloat16"),
    ("idp", 128, "bfloat16"), ("idn", 128, "bfloat16"), ("idk", 128, "float16"), ("uc1", 96, "bfloat16"), ("uc2", 96, "float16"),
    ("idw", 128, "float32"), ("idm", 128, "float16"), ("idh", 128, "float16"),
]:
    SCRATCH[_n] = ("sbuf", [128, _w], _d)
for _n in range(8):
    SCRATCH["bank%d" % _n] = ("psum", [128, 512], "float32")

LOADS = ["par", "qb", "clr", "clr2", "qi", "am", "th", "qdb", "qdi"]
SEMAPHORES = ["sv", "sa", "sp", "sgp"] + ["ld_" + x for x in LOADS] + ["st%d" % i for i in range(16)]
for _r in range(RO):
    SEMAPHORES += [x + "%d" % _r for x in ["ap", "lp", "db", "di", "nr"]]
    SEMAPHORES += [x + "%d_%d" % (_r, j) for x in ["aq", "lq"] for j in range(2)]

WHO = dict(names="mask", T8="a", T1="v", T2="a", T3="a", T5="v", upd="T", T7="v", G6="a", P6="a", fin="v")
CFG = dict(chunks=[dict(WHO, c0=0, k=32, ps=[(0, 0), (6, 256)], pe=[(3, 0), (3, 256)], ls=(6, 0), T2="ae", T3="av", T7="a"),
                   dict(WHO, c0=32, k=32, ps=[(1, 0)], pu=[(1, 0)], pe=[(4, 0)], ls=(7, 0), upd="G", names="rows", T1="a"),
                   dict(WHO, c0=64, k=32, ps=[(2, 0)], pe=[(3, 0)], ls=(5, 0), names="rows")],
           merge=("kp", "un", "wh"), near=1, stq="s", kp="v", lc=True,
           late=dict(qi=[("pr", 0)], qdb=[("wr", 0, 0)], qdi=[("wr", 0, 0)]))
ORDER = """
T5.0@4+3 c_n0+2 sl.0@0+3 un.1@0+2 tt.0@0+3 us.0@0+3 pn.0@0+3 c_half01+2 kp.1+3 T7.2+3 tt.1@4+4 hc.1+3 ed.1@0+3
sa.1@4+3 sl.0+3 c_half00+1 sd.1+3 ea.1+3 ed.1+3 ea.1@4+3 ea.2+3 ma.1@4+4 ea.2@4+3 sd.1@4+3 wu.0@4+3 ed.1@4+3 sd.2@0+3
sd.2+3 wc.1@0+3 sd.2@4+3 mb.1@4+4 ea.2@0+3 T3.1+3 l_am+1 T4.1@0+3 T4.1+3 T3.2+3 c_nr1+1 wc.1+3 T3.1@4+3 T3.2@0+3
wc.1@4+3 ed.2@4+3 ed.2+3 ed.2@0+3 T4.2@0+3 c_sum+2 wc.2+3 ea.0@0+2 wc.2@0+3 nr@0+2 styp0+5 di+4 sp_0+1 l_qi+2 sq_0_0+1
l_clr2+1 di@0+4 kp.1@0+1 sp@0+3 sl.2@4+4 tt.0+3 pn.1@4+4 T6.0@0+3 c_wcol+2 kp.0@0+1 uc.1@0+3 us.0+3 us.2@4+4 pn.0+3
T6.0+3 c_zc+2 c_oh1+1 sl.0@4+3 up.0@4+2 c_b1+2 bcp.0@4+2 c_idm+1 c_nr0 c_zero us.0@4+3 uc.1+3 c_zn+2 up.0+2 c_zp+2
c_oh2+1 T5.1@0+3 uc.2@0+3 u4.0+2 T5.1+3 c_idw+1 c_oh3+1 c_pk2+1 c_gcol+1 l_clr+2 l_par i_p l_qdb+2 sp+3 sq.0@0+3
styp1+5 i_u1+2 styp2+5 styq1+5 T4.2+3 sq.0+3 T4.1@4+3 T3.2@4+3 T8.0@4+2 T8.0+2 T8.0@0+1 P6.1@4+4 pn.0@4+4 uc.2+3
T5.2@0+3 u4.0@4+2 T5.2+3 c_pcol T1.0+2 T1.0@4+2 ma.1+3 uk.1@0+3 uk.2+3 uk.2@0+3 wu.1@0+3 wu.2@0+3 tt.2@4+4 ea.0@4+2
uk.1+3 wh.0@0+2 wu.1+3 sl.1+3 wu.2+3 sa.0@4+2 c_two wh.0@4+2 wh.0+2 wc.2@4+3 T6.2@4+4 pn.2@4+4 uh.0@0+2 c_rci sl.2+3
tt.1+3 pm0 c_idn+1 sl.1@0+3 sl.2@0+3 tt.2+3 c_b0+1 hc.0@0+2 c_n1+2 T6.0@4+3 uc.1@4+3 us.1+3 c_idk+1 tt.1@0+3 fin1+4
pn.1+3 pn.2+3 bT2.0@0+2 tt.2@0+3 T1.2@0+2 fin2+4 us.2+3 us.2@0+3 T5.1@4+3 uc.2@4+3 h4.1@4+2 uh.0@4+2 us.1@0+3 pn.1@0+3
c_rcol c_pk3+1 pn.2@0+3 bcp.0+2 hc.0@4+2 h4.1+2 T7.2@0+2 c_am2+1 uh.0+2 styq2+5 i_u2+1 nr+2 styq0+4 nr@4+2 l_qdi+2
db@0+3 i_16 i_143 T7.0@4+2 db+3 T7.0+2 G6.1@0+3 T4.2@4+3 G6.1+3 T7.0@0+1 T2.0@0+2 T2.0@4+2 uk.1@4+3 nm.1@4+2 nm.1+2
sa.0@0+2 c_idh+1 hc.0+2 T6.2@0+3 bT2.0@4+2 un.1@4+2 T6.2+3 bT2.0+2 c_idp T5.2@4+3 ea.0+2 bsa.0@4+2 sd.0@4+2 bsa.0@0+2
ed.0@0+2 bT4.0@4+2 l_qb sd.0@0+2 T1.1@0+2 sa.0+2 ma.1@0+3 T2.0+2 ed.0@4+2 bsd.0@4+2 bsa.0+2 mb.1+3 sd.0+2 ed.0+2
bsd.0+2 bsd.0@0+2 wu.1@4+3 sa.2@4+2 sa.2+2 wh.1@0+2 sl.1@4+3 bT3.0@4+2 bT3.0@0+2 T1.2@4+2 tt.0@4+3 T7.2@4+2 us.1@4+3
uh.1@0+2 c_one+1 c_zo+1 un.1+2 bcp.0@0 c_oh0 kp.0@4+2 kp.0+2 c_uc2+2 pm1 bT3.0+2 T3.0+2 T3.0@0+2 bT4.0+2 T4.0+2 T1.1+2
G6.1@4+3 bT4.0@0+2 T3.0@4+2 wc.0@0+2 sa.1@0+2 uk.2@4+3 sa.2@0+2 wc.0+2 wc.0@4+2 uk.0+2 mb.1@0+3 P6.1@0+3 T1.1@4+2
T4.0@0+2 T2.1@0+2 l_th P6.1+3 h4.1@0+1 hc.1@0+2 fin0+3 T1.0@0+1 uk.0@0+2 wh.1@4+2 nm.1@0+1 wu.2@4+3 T1.2+2 uc.0@4+2
uc.0+2 u4.0@0 uc.0@0+2 wh.1+2 uk.0@4+2 ea.1@0+2 sd.1@0+2 kp.1@4+2 T5.0+2 uh.1+2 uh.1@4+2 up.0@0 T5.0@0+2 hc.1@4+2
wu.0+2 T4.0@4+2 T2.1@4+2 wu.0@0+2 sa.1+2 T2.2@4+2 T2.2@0+2 T3.1@0+2 T2.1+2 T2.2+2
"""


def build_ops(g, T, topo, core, rank, cfg):
    ops = []

    def op(name, eng, kind, reads, writes, fn, sem=None, banks=()):
        ops.append(dict(name=name, eng=eng, kind=kind, reads=reads, writes=writes, fn=fn, sem=sem, banks=banks))

    vec, act, pe = g.vector, g.scalar, g.tensor
    W = [T["w%d" % r] for r in range(RO)]
    PW = [T["pw%d" % r] for r in range(RO)]
    own0 = OFF + B * rank
    CH = cfg["chunks"]
    BORDER = [i for i, ch in enumerate(CH) if ch["c0"] < 32]
    INNER = [i for i, ch in enumerate(CH) if ch["c0"] >= 32]
    rows = any(ch["names"] == "rows" for ch in CH)
    maski = any(CH[i]["names"] == "mask" for i in INNER)

    def dma(name, eng, out, in_, reads, writes, sem):
        q = g.sync if eng == "s" else g.scalar
        op(name, eng, "dma", reads, writes, lambda: q.dma_start(out, in_), sem)

    def load(name, eng, out, in_, writes):
        dma("l_" + name, eng, out, in_, cfg["late"].get(name, []), writes, "ld_" + name)

    def gp(name, w, fn):
        op(name, "g", "iota", [], [w], fn)

    def vs(name, reads, writes, fn, banks=()):
        op(name, "v", "op", reads, writes, fn, None, banks)

    def ac(name, reads, writes, fn, banks=()):
        op(name, "a", "op", reads, writes, fn, None, banks)

    def mm(name, reads, bank, fn):
        op(name, "p", "mm", reads, [], fn, None, (bank,))

    def affine(name, e, out, in_, scale, bias, reads, writes, banks=()):
        if e == "v":
            vs(name, reads, writes, lambda: vec.tensor_scalar(out, in_, scale, bias, ALU.mult, ALU.add), banks)
        else:
            ac(name, reads, writes, lambda: act.activation(out, in_, AF.Copy, bias=bias, scale=scale), banks)

    def gather(name, e, out, win, off, reads, writes):
        if e == "v":
            op(name, "v", "gat", reads, writes, lambda: vec.tensor_copy(out, win.indirect(off)))
        else:
            op(name, "a", "gat", reads, writes, lambda: act.activation(out, win.indirect(off), AF.Copy))

    def psum(place, a, n):
        return T["bank%d" % place[0]][:, place[1] + a:place[1] + a + n]

    others = [c for c in T.cores if c != core]
    near = [c for c in others if c in topo.cores_of(core)]
    far = [c for c in others if c not in near]
    fe = topo.engines(core, far[0])
    eng = {}
    for i, c in enumerate(far):
        k = len(fe) // len(far)
        eng[c] = fe[i * k:(i + 1) * k]
    for c in near:
        eng[c] = [e for e in topo.engines(core, c) if e not in fe][::cfg["near"]]
    total = sum(len(x) for x in eng.values())

    def send(name, ap, rsem, lsem, reads, arrives):
        def fn():
            trs = []
            for c in far + near:
                rid, pid = topo.addr(c, core)
                trs.append(RemoteDMATransfer(dst_ids=[DstId(rid=rid, pnc=pid)], dma_engine_mask=sum(1 << e for e in eng[c]),
                                             remote_sem=T.sem[rsem], src=ap, dst=ap))
            return g.remote_dma_fused(trs, local_sem=T.sem[lsem])
        op(name, "g", "send", reads, arrives, fn, (rsem, lsem, total))

    def own(r, c0, k):
        if r == RO:
            return T.fin[:, 16 * c0:16 * (c0 + k)]
        a = (own0 if c0 < 32 else INN - B) + 16 * c0
        return W[r][:, a:a + 16 * k]

    def pm(r, c0, k):
        if r == RO:
            return T.pfin[:, c0:c0 + k]
        a = (32 * rank if c0 < 32 else 96) + c0
        return PW[r][:, a:a + k]

    def wk(r, ci):
        return [("w", r, ci, 0), ("w", r, ci, 1)]

    load("par", "s", T.pari[:], T.par[:], ["pari"])
    load("qb", "a", W[0][:, own0:own0 + B], T.q[:, 0:B], [x for i in BORDER for x in wk(0, i)])
    vs("pm0", ["pari"], [("pw", 0, i) for i in BORDER], lambda: vec.tensor_scalar(pm(0, 0, 32), T.pari[:, 0:32], -float(CEN), None, ALU.add))
    send("sp_0", pm(0, 0, 32), "ap0", "lp0", [("pw", 0, i) for i in BORDER], [("pr", 0)])
    send("sq_0_0", own(0, 0, 32), "aq0_0", "lq0_0", [x for i in BORDER for x in wk(0, i)], [("wr", 0, 0), ("wr", 0, 1)])
    vs("pm1", ["pari"], [("pw", 0, i) for i in INNER], lambda: vec.tensor_scalar(pm(0, 32, 64), T.pari[:, 32:96], -float(CEN), None, ALU.add))
    load("qi", "s", W[0][:, INN:DUP], T.q[:, B:V], [x for i in INNER for x in wk(0, i)])
    load("am", "a", T.am[:], T.amat[:], ["am"])
    load("clr", "s", T.clrs[:, 0:C // 2], T.clr[:, 0:C // 2], ["clrs"])
    load("clr2", "s", T.clrs[:, C // 2:C], T.clr[:, C // 2:C], ["clrs2"])
    load("th", "a", T.thi[:], T.th[:], ["thi"])
    load("qdb", "s", W[0][:, 0:B], T.q[:, 0:B], [("wd", 0, 0)])
    load("qdi", "s", W[0][:, DUP:WW], T.q[:, B:V], [("wd", 0, 1)])

    gp("i_p", "pci", lambda: g.iota(T.pci[:], [[0, 1]], 0, 1))
    gp("i_16", "x16", lambda: g.iota(T.x16[:], [[0, 16], [1, 16]], 0, 0, allow_small_or_imprecise_dtypes=True))
    gp("i_143", "x143", lambda: g.iota(T.x143[:], [[1, 144]], -15, 0, allow_small_or_imprecise_dtypes=True))
    gp("i_u1", "uc1b", lambda: g.iota(T.uc1[:, 0:32], [[16, 32]], 0, 0, allow_small_or_imprecise_dtypes=True))
    gp("i_u2", "uc1i", lambda: g.iota(T.uc1[:, 32:96], [[16, 64]], NAMES, 0, allow_small_or_imprecise_dtypes=True))
    vs("c_two", [], ["two"], lambda: vec.memset(T.two[:], 2.0))
    vs("c_zero", [], ["zero"], lambda: vec.memset(T.zero[:], 0.0))
    vs("c_one", [], ["one"], lambda: vec.memset(T.one[:], 1.0))
    vs("c_pk2", ["two", "zero"], ["pk2"], lambda: vec.tensor_tensor_scan(T.pk2[:], T.two[:], T.zero[:], 0.25, ALU.mult, ALU.add))
    vs("c_rci", ["pci"], ["rci"], lambda: vec.tensor_scalar(T.rci[:], T.pci[:], 15, None, ALU.bitwise_and))
    vs("c_rcol", ["rci"], ["rcol"], lambda: vec.tensor_copy(T.rcol[:], T.rci[:]))
    vs("c_pcol", ["pci"], ["pcol"], lambda: vec.tensor_copy(T.pcol[:], T.pci[:]))
    vs("c_gcol", ["pcol", "rcol"], ["gcol"], lambda: vec.tensor_tensor(T.gcol[:], T.pcol[:], T.rcol[:], ALU.subtract))
    vs("c_oh0", ["x16", "rcol"], ["oh0"], lambda: vec.tensor_scalar(T.oh[:, 0:256], T.x16[:], T.rcol[:], None, ALU.is_equal))
    vs("c_oh1", ["oh0"], ["oh1"], lambda: vec.tensor_copy(T.oh[:, 256:512], T.oh[:, 0:256]))
    vs("c_oh2", ["oh0", "oh1"], ["oh2"], lambda: vec.tensor_copy(T.oh[:, 512:1024], T.oh[:, 0:512]))
    vs("c_oh3", ["oh0", "oh1", "oh2"], ["ohb"], lambda: vec.tensor_copy(T.oh[:, 1024:2048], T.oh[:, 0:1024]))
    if maski:
        ac("c_oh4", ["oh0", "oh1", "oh2"], ["ohi"], lambda: act.activation(T.oh[:, 2048:3072], T.oh[:, 0:1024], AF.Copy))
    vs("c_pk3", ["pk2", "oh0"], ["pk3"], lambda: vec.tensor_tensor(T.pk3[:], T.pk2[:], T.oh[:, 0:16], ALU.mult))
    vs("c_wcol", ["pk3"], ["wcol"], lambda: vec.tensor_reduce(T.wcol[:], T.pk3[:, 0:12], AxisListType.X, ALU.add))
    vs("c_zo", ["x143", "gcol"], ["zo"], lambda: vec.tensor_scalar(T.zo[:], T.x143[:], T.gcol[:], None, ALU.is_equal))
    vs("c_zc", ["x143", "gcol", "wcol"], ["zc"],
       lambda: vec.tensor_scalar(T.zc[:], T.x143[:], T.gcol[:], T.wcol[:], ALU.is_equal, ALU.mult))
    vs("c_zp", ["zo"], ["zp"], lambda: vec.tensor_scalar(T.zp[:], T.zo[:], BIG, None, ALU.mult))
    vs("c_zn", ["zo"], ["zn"], lambda: vec.tensor_scalar(T.zn[:], T.zo[:], -BIG, None, ALU.mult))
    vs("c_idp", ["x143", "pcol"], ["idp"], lambda: vec.tensor_scalar(T.idp[:], T.x143[:, 15:143], T.pcol[:], None, ALU.is_equal))
    vs("c_idk", ["idp"], ["idk"], lambda: vec.tensor_scalar(T.idk[:], T.idp[:], PK, None, ALU.mult))
    if any(ch["T2"].strip("e") for ch in CH):
        vs("c_idn", ["idp"], ["idn"], lambda: vec.tensor_scalar(T.idn[:], T.idp[:], -1.0, None, ALU.mult))
    if any("e" in ch["T2"] for ch in CH):
        vs("c_am2", ["am"], ["am2"], lambda: vec.tensor_scalar(T.am2[:], T.am[:], 2.0, None, ALU.mult))
    vs("c_uc2", ["uc1b", "uc1i", "rcol"], ["uc2"], lambda: vec.tensor_scalar(T.uc2[:], T.uc1[:], -MID, T.rcol[:], ALU.add, ALU.add))
    vs("c_idh", ["idp"], ["idh"], lambda: vec.tensor_copy(T.idh[:], T.idp[:]))
    if rows:
        vs("c_nr0", [], ["nr0"], lambda: vec.memset(T.nr[:, 0:NAMES // 2], 0.0))
        ac("c_nr1", ["nr0"], ["nr"], lambda: act.activation(T.nr[:, NAMES // 2:NAMES], T.nr[:, 0:NAMES // 2], AF.Copy))
        vs("c_idw", ["idp"], ["idw"], lambda: vec.tensor_scalar(T.idw[:], T.idp[:], float(LW), None, ALU.mult))
        vs("c_idm", ["idp"], ["idm"], lambda: vec.tensor_scalar(T.idm[:], T.idp[:], -16.0 * LW, None, ALU.mult))
    sb = CH[INNER[0]]["ls"][0]
    vs("c_b0", ["thi"], ["b0"], lambda: vec.tensor_scalar(T.b0[:], T.thi[:], -1.0, -0.5, ALU.mult, ALU.add))
    mm("c_sum", ["am", "one"], sb, lambda: pe.matmul(T["bank%d" % sb][:, 500:501], T.am[:], T.one[:], True, True))
    vs("c_b1", ["b0"], ["b1"], lambda: vec.tensor_scalar(T.b1[:], T["bank%d" % sb][:, 500:501], -256.0, T.b0[:], ALU.mult, ALU.add), (sb,))
    if any("v" in ch["T3"] for ch in CH):
        vs("c_n1", ["b1", "pk2"], ["n1"], lambda: vec.tensor_scalar(T.nth[:, 1:RO], T.pk2[:, 2:RO + 1], T.b1[:], -1.0, ALU.mult, ALU.mult))
        vs("c_n0", ["b0"], ["n0"], lambda: vec.tensor_scalar(T.nth[:, 0:1], T.b0[:], -1.0, None, ALU.mult))
    for i, ch in enumerate(CH):
        if len(set(ch["T3"])) > 1:
            for j in range(2):
                ap = T.half[:, ch["c0"] + j * ch["k"] // 2:ch["c0"] + (j + 1) * ch["k"] // 2]
                vs("c_half%d%d" % (i, j), [], [("half", i)], lambda ap=ap, x=2048.0 * (ch["T3"][j] == "a"): vec.memset(ap, x))

    def span(cis):
        c0, k = CH[cis[0]]["c0"], sum(CH[i]["k"] for i in cis)
        return c0, k, slice(c0, c0 + k)

    def lists(r, cis, step):
        c0, k, cs = span(cis)
        t, p, pk = "_%d_%d" % (r, cis[0]), pm(r, c0, k), [("pw", r, i) for i in cis]
        if step == "kp":
            affine("kp" + t, cfg["kp"], T.keep[:, cs], p, PK + 1, PK * (CEN - MID + (OFF if c0 < 32 else 0)), pk, [("keep", i) for i in cis])
        elif step == "up" and any(CH[i]["names"] == "mask" for i in cis):
            vs("up" + t, pk, [("up", i) for i in cis], lambda: vec.tensor_scalar(T.up[:, cs], p, float(CEN), None, ALU.add))
        elif step == "u4" and any(CH[i]["names"] == "mask" for i in cis):
            vs("u4" + t, pk, [("u4", i) for i in cis],
               lambda: vec.tensor_scalar(T.u4[:, cs], p, 1.0 / 16, CEN / 16 - 15.0 / 32, ALU.mult, ALU.add))
        elif step == "un" and any(CH[i]["names"] == "rows" for i in cis):
            ls = CH[cis[-1]]["ls"]
            o = psum(ls, 192, k)
            vs("h4" + t, pk, [("h4", cis[0])],
               lambda: vec.tensor_scalar(T.h4[:, cs], p, 1.0 / 16, CEN / 16 + 1100 - 15.0 / 32, ALU.mult, ALU.add))

            def place():
                pe.matmul(o, T.idw[:], p, True, False)
                pe.matmul(o, T.idm[:], T.h4[:, cs], False, False)
                return pe.matmul(o, T.idh[:], T.h4[:, cs], False, True)
            mm("nm" + t, pk + [("h4", cis[0]), "idw", "idm", "idh"], ls[0], place)
            vs("un" + t, [], [("un", i) for i in cis],
               lambda: vec.tensor_scalar(T.un[:, cs], o, 1.0 * CEN * LW + 1100.0 * (16 * LW - 1), None, ALU.add), (ls[0],))

    def parents(r, cis):
        c0, k, cs = span(cis)
        t = "_%d_%d" % (r, cis[0])
        last = r + 1 == RO
        vs("tt" + t, [("sl", i) for i in cis], [("tt", cis[0])],
           lambda: vec.tensor_scalar(T.tt[:, cs], T.sl[:, cs], SNAP, -SNAP - (CEN if last else 0), ALU.add, ALU.add) if not last else
           vec.tensor_scalar(T.tt[:, cs], T.us[:, cs], PK, -PK * MID - CEN, ALU.mult, ALU.add))
        if last:
            ops[-1]["reads"] = [("us", i) for i in cis]
        vs("pn" + t, [("tt", cis[0])] + [("sl", i) for i in cis], [("pw", r + 1, i) for i in cis],
           lambda: vec.tensor_tensor(pm(r + 1, c0, k), T.sl[:, cs], T.tt[:, cs], ALU.subtract))
        if last:
            dma("styp%d" % cis[0], cfg["stq"], T.yp[:, cs], pm(RO, c0, k), [("pw", RO, i) for i in cis], [], "st%d" % (8 + cis[0]))

    def block_round(r, ci, stage, together):
        ch = dict(CH[ci], **CH[ci].get("at", {}).get(r, {}))
        k, c0, ls = ch["k"], ch["c0"], ch["ls"]
        inner = c0 >= 32
        t = "_%d_%d" % (r, ci)
        cs, wn = slice(c0, c0 + k), (NAMES if inner else M)
        seen = list(range(len(CH))) if inner else BORDER
        wkeys = [x for i in seen for x in wk(r, i)] + [("wr", r, 0), ("wr", r, 1)]
        pkeys = [("pw", r, i) for i in seen] + [("pr", r)]
        inv, bias = 1.0 / 2 ** r, (255.75 if r == 0 else -0.25 * 2 ** r)
        win = W[r][:, OFF:OFF + wn]
        wide = W[r][:, OFF:WW] if inner else W[r][:, 0:INN]

        def pieces(s):
            h = k // len(s)
            return [dict(x="b" if j else "", e=s[j], j=j, n=16 * h, cs=slice(c0 + j * h, c0 + (j + 1) * h),
                         bs=slice(16 * (c0 + j * h), 16 * (c0 + (j + 1) * h)), a=own(r, c0 + j * h, h), new=own(r + 1, c0 + j * h, h),
                         js=[j] if len(s) > 1 else [0, 1]) for j in range(len(s))]

        def keys(b, h=None):
            return [(b, ci, j) for j in (h["js"] if h else [0, 1])]

        def mine(q, h):
            return [("w", q, ci, j) for j in h["js"]]

        def over_groups(out, z, src, first, last, n=k):
            for j in range(16):
                ins = pe.matmul(out, T[z][:, 15 - j:143 - j], src[:, 16 * c0 + j:16 * (c0 + n):16], first and j == 0, last and j == 15)
            return ins

        def names(h):
            op(h["x"] + "T1" + t, "v", "gat", pkeys + [("u4", ci)] + keys("msk", h), keys("cand", h),
               lambda: vec.tensor_tensor(T.cand[:, h["bs"]], PW[r][:, 0:wn // 16].indirect(T.u4[:, h["cs"]]), T.msk[:, h["bs"]], ALU.mult))

        banks = pieces(ch["T3"])
        for h in banks:
            h["ps"], h["pd"], h["diff"] = ch["ps"][h["j"]], ch["pe"][h["j"]], ch["T2"][min(h["j"], len(ch["T2"]) - 1)] == "e"

        def sa(h):
            mm(h["x"] + "sa" + t, ["am", "am2"] + mine(r, h), h["ps"][0],
               lambda: pe.matmul(psum(h["ps"], 0, h["n"]), (T.am2 if h["diff"] else T.am)[:], h["a"], True, False))

        def grand(h):
            d = T.dd[:, h["bs"]]
            if h["e"] == "e":
                if ch.get("dup"):
                    a2, src = W[r][:, DUP - B + h["bs"].start:DUP - B + h["bs"].stop], [("wd", r, 1)]
                else:
                    a2, src = T.aa[:, h["bs"]], keys("aa", h)
                    vs(h["x"] + "cp" + t, mine(r, h), src, lambda: vec.tensor_copy(a2, h["a"]))
                op(h["x"] + "T2" + t, "v", "gat", wkeys + [("uh", ci)] + src, keys("dd", h),
                   lambda: vec.tensor_tensor(d, win.indirect(T.uh[:, h["cs"]]), a2, ALU.subtract))
            else:
                gather(h["x"] + "T2" + t, h["e"], d, win, T.uh[:, h["cs"]], wkeys + [("uh", ci)], keys("dd", h))

        def bits(h):
            x, d, ps, pd = h["x"], T.dd[:, h["bs"]], psum(h["ps"], 0, h["n"]), psum(h["pd"], 0, h["n"])
            mm(x + "sd" + t, ["am"] + keys("dd", h), h["ps"][0], lambda: pe.matmul(ps, T.am[:], d, False, True))
            if not h["diff"]:
                mm(x + "ea" + t, ["idp"] + mine(r, h), h["pd"][0], lambda: pe.matmul(pd, T.idp[:], h["a"], True, False))
                mm(x + "ed" + t, ["idn"] + keys("dd", h), h["pd"][0], lambda: pe.matmul(pd, T.idn[:], d, False, True))
            if h["e"] == "a":
                th = T.b0 if r == 0 else T.b1
                ac(x + "T3" + t, ["b0", "b1"], keys("sg", h),
                   lambda: act.activation(T.sg[:, h["bs"]], ps, AF.Sign, bias=th[:], scale=inv), (h["ps"][0],))
            else:
                vs(x + "T3" + t, ["n0", "n1"], keys("sg", h),
                   lambda: vec.tensor_scalar(T.sg[:, h["bs"]], ps, T.nth[:, r:r + 1], 2.0, ALU.is_gt, ALU.mult), (h["ps"][0],))
            if h["diff"]:
                ac(x + "T4" + t, keys("dd", h), keys("ae", h), lambda: act.activation(T.ae[:, h["bs"]], d, AF.Abs, scale=inv))
            else:
                ac(x + "T4" + t, [], keys("ae", h), lambda: act.activation(T.ae[:, h["bs"]], pd, AF.Abs, scale=inv), (h["pd"][0],))

        def room(h):
            op(h["x"] + "T5" + t, "v", "gat", ["clrs", "clrs2", ("uc", ci)] + keys("ae", h), keys("viol", h),
               lambda: vec.tensor_tensor(T.viol[:, h["bs"]], T.clrs[:].indirect(T.uc[:, h["cs"]]), T.ae[:, h["bs"]], ALU.is_lt))

        def quarter(h):
            return (T.ah if ch["T7"][h["j"]] == "v" else T.ab)[:, h["bs"]]

        def update(h):
            x, j, rd = h["x"], h["j"], wkeys + [("wd", r, int(inner)), ("us", ci)]
            if h["e"] == "T":
                op(x + "T6" + t, "v", "gat", rd + keys("ab", h), mine(r + 1, h),
                   lambda: vec.tensor_tensor(h["new"], wide.indirect(T.us[:, h["cs"]]), quarter(h), ALU.add))
                return
            ps = ch["pu"][j]
            q = psum(ps, 0, h["n"])
            mm(x + "ma" + t, ["idp"] + mine(r, h), ps[0], lambda: pe.matmul(q, T.idp[:], h["a"], True, False))
            gather(x + "G6" + t, ch["G6"][j], T.gg[:, h["bs"]], wide, T.us[:, h["cs"]], rd, keys("gg", h))
            mm(x + "mb" + t, ["idp"] + keys("gg", h), ps[0], lambda: pe.matmul(q, T.idp[:], T.gg[:, h["bs"]], False, True))
            affine(x + "P6" + t, ch["P6"][j], h["new"], q, 1.0, bias, [], mine(r + 1, h), (ps[0],))

        if stage == "names":
            for h in pieces(ch["upd"]):
                if h["e"] == "T":
                    affine(h["x"] + "T7" + t, ch["T7"][h["j"]], quarter(h), h["a"], 1.0, bias, mine(r, h), keys("ab", h))
            if ch["names"] == "mask":
                for h in pieces(ch["T8"]):
                    gather(h["x"] + "T8" + t, h["e"], T.msk[:, h["bs"]], T.oh[:, 0:wn], T.up[:, h["cs"]],
                           ["oh0", "oh1", "oh2", "ohb", ("up", ci)] + (["ohi"] if inner else []), keys("msk", h))
                for h in pieces(ch["T1"]):
                    names(h)
            else:
                for h in pieces(ch["T1"]):
                    gather(h["x"] + "T1" + t, h["e"], T.cand[:, h["bs"]], T.nr[:], T.un[:, h["cs"]], ["nr", ("un", ci)], keys("cand", h))
            for h in banks:
                if h["ps"][0] != ls[0]:
                    sa(h)
            return
        lc = ch["ps"][0] if cfg["lc"] else (ls[0], ls[1] + k)
        cd, u = psum(lc, 0, k), psum(ls, 0, k)
        if together[0] == ci:
            _, kk, cc = span(together)
            hm = psum(ls, 128, kk)
            mm("wh" + t, ["zo"] + [("cand", i, j) for i in together for j in (0, 1)], ls[0],
               lambda: over_groups(hm, "zo", T.cand, True, True, kk))
            vs("uh" + t, [], [("uh", i) for i in together],
               lambda: vec.tensor_scalar(T.uh[:, cc], hm, float(CEN), None, ALU.add), (ls[0],))
            vs("hc" + t, [], [("hs", i) for i in together], lambda: vec.tensor_copy(T.hs[:, cc], hm), (ls[0],))
        for h in banks:
            if h["ps"][0] == ls[0]:
                sa(h)
        for h in pieces(ch["T2"]):
            grand(h)
        for h in banks:
            bits(h)
        mixed = len(set(ch["T3"])) > 1

        def code():
            if mixed:
                pe.matmul(cd, T.idp[:], T.half[:, cs], True, False)
            return over_groups(cd, "zc", T.sg, not mixed, True)
        mm("wc" + t, ["zc", ("half", ci)] + keys("sg"), lc[0], code)
        vs("uc" + t, [], [("uc", ci)],
           lambda: vec.tensor_scalar(T.uc[:, cs], cd, -0.25 if mixed else 2047.5 if ch["T3"][0] == "a" else 0.0, None, ALU.add), (lc[0],))

        def granted():
            pe.matmul(u, T.idk[:], T.uc2[:, cs], True, False)
            return pe.matmul(u, T.idh[:], T.hs[:, cs], False, False)
        mm("uk" + t, ["idk", "uc2", "idh", ("hs", ci)], ls[0], granted)
        for h in pieces(ch["T5"]):
            room(h)
        z = "zn" if inner else "zp"
        mm("wu" + t, [z] + keys("viol"), ls[0], lambda: over_groups(u, z, T.viol, False, True))
        vs("sl" + t, [("keep", ci)], [("sl", ci)],
           lambda: vec.tensor_tensor(T.sl[:, cs], u, T.keep[:, cs], ALU.max if inner else ALU.min), (ls[0],))
        vs("us" + t, [("sl", ci)], [("us", ci)], lambda: vec.tensor_scalar(T.us[:, cs], T.sl[:, cs], 1 / PK, MID, ALU.mult, ALU.add))
        for h in pieces(ch["upd"]):
            update(h)
        if r + 1 == RO:
            for h in pieces(ch["fin"]):
                s = "%s%d" % (h["x"], ci)
                affine("fin" + s, h["e"], T.yqs[:, h["bs"]], T.fin[:, h["bs"]], 1.0 / 2 ** RO, -128.0, mine(RO, h), keys("yq", h))
                dma("styq" + s, "s", T.yq[:, h["bs"]], T.yqs[:, h["bs"]], keys("yq", h), [], "st%d" % (2 * ci + h["j"]))
        elif not inner:
            for h in pieces(ch["upd"]):
                send(h["x"] + "sq_%d_%d" % (r + 1, ci), h["new"], "aq%d_%d" % (r + 1, h["j"]), "lq%d_%d" % (r + 1, h["j"]),
                     mine(r + 1, h), [("wr", r + 1, j) for j in h["js"]])

    def sets(step, cis):
        return [cis] if step in cfg["merge"] or cis is BORDER else [[i] for i in cis]

    for r in range(RO):
        if rows:
            dma("nr_%d" % r, "s", T.nr[0:128:16, :], PW[r][:], [("pw", r, i) for i in range(len(CH))] + [("pr", r)], ["nr0", "nr"], "nr%d" % r)
        for cis in (BORDER, INNER):
            for step in ("kp", "up", "u4", "un"):
                for x in sets(step, cis):
                    lists(r, x, step)
            for stage in ("names", "rest"):
                for x in sets("wh", cis):
                    for ci in x:
                        block_round(r, ci, stage, x)
            for x in sets("pn", cis):
                parents(r, x)
            if r + 1 == RO:
                continue
            if cis is BORDER:
                send("sp_%d" % (r + 1), pm(r + 1, 0, 32), "ap%d" % (r + 1), "lp%d" % (r + 1), [("pw", r + 1, i) for i in BORDER], [("pr", r + 1)])
                dma("db_%d" % r, "s", W[r + 1][:, 0:B], own(r + 1, 0, 32),
                    [x for i in BORDER for x in wk(r + 1, i)] + [("wr", r + 1, 0), ("wr", r + 1, 1)], [("wd", r + 1, 0)], "db%d" % r)
            else:
                dma("di_%d" % r, "s", W[r + 1][:, DUP:WW], W[r + 1][:, INN:DUP], [x for i in INNER for x in wk(r + 1, i)],
                    [("wd", r + 1, 1)], "di%d" % r)

    writer, readers, turn = {}, {}, {}
    for i, o in enumerate(ops):
        d = set()
        for x in o["reads"]:
            if x in writer:
                d.add(writer[x])
        for x in o["writes"]:
            if x in writer:
                d.add(writer[x])
            d.update(readers.get(x, []))
        for b in o["banks"]:
            e, now, before = turn.get(b, (None, [], []))
            if e != o["eng"]:
                now, before = [], now
            d.update(before)
            if o["eng"] == "p":
                d.update(now[-1:])
            turn[b] = (o["eng"], now + [i], before)
        d.discard(i)
        o["deps"] = sorted(d)
        for x in o["reads"]:
            readers.setdefault(x, []).append(i)
        for x in o["writes"]:
            writer[x] = i
            readers[x] = []
    return ops


def step_of(name):
    p = name.split("_")
    if len(p) == 1 or p[0] in ("c", "i", "l") or name in ("sp_0", "sq_0_0"):
        return name, (RO - 1 if name[:3] in ("fin", "sty") else 0)
    return ".".join(p[:1] + p[2:]), int(p[1]) - (p[0] in ("sp", "sq", "bsq"))


def issue_order(ops, order):
    steps = [(x.split("+")[0], int((x + "+0").split("+")[1])) for x in order.split()]
    listed = [s for s, lag in steps]
    index = {}
    for i, o in enumerate(ops):
        s, r = step_of(o["name"])
        index[(s + "@%d" % r if s + "@%d" % r in listed else s, r)] = i
    return [index[(s, t - lag)] for t in range(2 * RO) for s, lag in steps if (s, t - lag) in index]


def rank_program(g, core, T, topo):
    rank = T.rank_of(core)
    if rank is None:
        return
    ops = build_ops(g, T, topo, core, rank, CFG)
    order = issue_order(ops, ORDER) if ORDER else list(range(len(ops)))
    queue = {"v": g.vector, "a": g.scalar, "p": g.tensor, "s": g.sync, "g": g}
    esem = {"v": "sv", "a": "sa", "p": "sp", "g": "sgp"}
    count, token, seen, ends = {}, {}, {}, {}
    for i in order:
        o = ops[i]
        e = o["eng"]
        need = {}
        for d in o["deps"]:
            if e == "p" and ops[d]["eng"] == "p":
                continue
            s, v = token[d]
            need[s] = max(need.get(s, 0), v)
        for s, v in need.items():
            if seen.get((e, s), 0) < v:
                queue[e].wait_ge(T.sem[s], v)
                seen[(e, s)] = v
        ins = o["fn"]()
        if o["kind"] == "dma":
            ins.then_inc(T.sem[o["sem"]], 16)
            token[i] = (o["sem"], 16)
        elif o["kind"] == "send":
            token[i] = (o["sem"][0], o["sem"][2])
            ends[o["sem"][1]] = o["sem"][2]
        else:
            count[e] = count.get(e, 0) + 1
            ins.then_inc(T.sem[esem[e]], 1)
            token[i] = (esem[e], count[e])
        ends[token[i][0]] = token[i][1]
    for s, v in ends.items():
        if not any(k[1] == s and x >= v for k, x in seen.items()):
            g.wait_ge(T.sem[s], v)
